import numpy as np
import ml_dtypes


def mxq(x, axis, fmt="e4m3"):
    dtype, down = {"e4m3": (ml_dtypes.float8_e4m3fn, 7), "e5m2": (ml_dtypes.float8_e5m2, 14)}[fmt]
    v = np.moveaxis(np.asarray(x, np.float32).astype(ml_dtypes.bfloat16).astype(np.float64), axis, -1)
    blocks = v.reshape(v.shape[:-1] + (-1, 32))
    amax = np.abs(blocks).max(-1, keepdims=True)
    byte = np.maximum(np.where(amax > 0, np.frexp(amax)[1] - 1 + 127, 0) - down, 1)
    scale = np.exp2(byte - 127.0)
    codes = (blocks / scale).astype(np.float32).astype(dtype).astype(np.float64)
    return np.moveaxis((codes * scale).reshape(v.shape), -1, axis)


WIDE = False


def mx_kscale(k):
    if not WIDE:
        return np.ones(k)
    levels = np.array([10, -10, 5, -5, 0])
    if k % 512:
        return np.exp2(np.random.permutation(np.resize(levels, k // 32))).repeat(32)
    a = np.empty((k // 512, 16))
    for p in range(k // 512):
        a[p, :8] = np.random.permutation(np.resize(levels, 8))
        for g in range(8):
            far = levels[np.abs(levels - a[p, g]) >= 10]
            a[p, g + 8] = far[np.random.randint(len(far))]
    return np.exp2(a.ravel()).repeat(32)


def f64(x):
    return np.asarray(x).astype(np.float64)


def striped(idx):
    return np.tile(idx.reshape(-1, 16).T, (8, 1)).astype(np.uint16)


def unstriped(offs):
    return offs[:16].T.reshape(-1).astype(np.int64)


E2M1 = np.array([0.0, 0.5, 1.0, 1.5, 2.0, 3.0, 4.0, 6.0, -0.0, -0.5, -1.0, -1.5, -2.0, -3.0, -4.0, -6.0])


def pack_weight(w, fmt):
    k, n = w.shape
    w = f64(np.asarray(w, np.float32).astype(ml_dtypes.bfloat16)).reshape(k // 32, 32, n)
    amax = np.abs(w).max(1)
    if fmt == "e4m3":
        byte = np.frexp(amax)[1] - 1 + 127 - 7
    else:
        mant, ex = np.frexp(amax / 6.0)
        byte = np.where(mant > 0.5, ex, ex - 1) + 127
    byte = np.clip(np.where(amax > 0, byte, 1), 1, 254)
    scaled = (w * np.exp2(127.0 - byte)[:, None, :]).reshape(k, n).astype(np.float32)
    by_word = np.ascontiguousarray(scaled.reshape(k // 512, 128, 4, n).transpose(0, 1, 3, 2))
    if fmt == "e4m3":
        words = by_word.astype(ml_dtypes.float8_e4m3fn).view(np.uint8)
    else:
        c = by_word.astype(ml_dtypes.float4_e2m1fn).view(np.uint8) & 0xF
        words = (c[..., 0::2] | (c[..., 1::2] << 4)).reshape(k // 512, 128, 2 * n)
    return np.ascontiguousarray(words), np.ascontiguousarray(byte.astype(np.uint8).reshape(k // 512, 16, n))


def unpack_weight(words, scales, fmt):
    g, _, n = scales.shape
    words = np.ascontiguousarray(words).reshape(g, 128, n, -1)
    if fmt == "e4m3":
        vals = words.view(ml_dtypes.float8_e4m3fn).astype(np.float64)
    else:
        nib = np.empty((g, 128, n, 4), np.uint8)
        nib[..., 0::2] = words & 0xF
        nib[..., 1::2] = words >> 4
        vals = E2M1[nib]
    vals = vals * np.repeat(np.exp2(scales.astype(np.float64) - 127.0), 8, axis=1)[..., None]
    return vals.transpose(0, 1, 3, 2).reshape(g * 512, n)


def gelu(v):
    return 0.5 * v * (1.0 + np.tanh(np.sqrt(2.0 / np.pi) * (v + 0.044715 * v**3)))


K, K1, K2, H, T, S, T2, S2 = 1536, 512, 1024, 1024, 4096, 1024, 2048, 1024

def setup_inputs():
    n = np.random.standard_normal
    s = mx_kscale(K)[:, None]
    u = mx_kscale(H)[:, None]
    tab_words, tab_scales = pack_weight(n((K, T)) * s, "e4m3")
    tab2_words, tab2_scales = pack_weight(2.0 * n((H, T2)) / np.sqrt(H) / u, "e4m3")
    w1 = n((K1, H)) / np.sqrt(K) / s[:K1] * u.T
    w4_words, w4_scales = pack_weight(n((K2, H)) / np.sqrt(K) / s[K1:] * u.T, "e2m1")
    return {
        "tab_words": tab_words, "tab_scales": tab_scales,
        "offs": striped(np.random.permutation(T)[:S]),
        "tab2_words": tab2_words, "tab2_scales": tab2_scales,
        "offs2": striped(np.random.permutation(T2)[:S2]),
        "w1": w1.astype(np.float32),
        "w4_words": w4_words, "w4_scales": w4_scales,
        "b1": (0.5 * n(H) * u[:, 0]).astype(np.float32),
        "b2": (0.7 * n(S2) - 0.5).astype(np.float32),
    }

def reference(tab_words, tab_scales, offs, tab2_words, tab2_scales, offs2, w1, w4_words, w4_scales, b1, b2):
    v = unpack_weight(tab_words, tab_scales, "e4m3")[:, unstriped(offs)]
    v2 = unpack_weight(tab2_words, tab2_scales, "e4m3")[:, unstriped(offs2)]
    w1q = mxq(f64(w1), 0, "e4m3")
    w4 = unpack_weight(w4_words, w4_scales, "e2m1")
    a = w1q.T @ v[:K1] + w4.T @ v[K1:]
    h = np.maximum(a + f64(b1)[:, None], 0.0)
    hq = mxq(h, 0, "e4m3")
    z = (v2.T @ hq) + f64(b2)[:, None]
    return 1.0 / (1.0 + np.exp(-z))

@@ -1,0 +1,282 @@
+from contextlib import ExitStack
+
+import concourse.mybir as mybir
+from concourse.masks import make_identity
+
+K1, K2, H = 512, 1024, 1024
+T, S = 4096, 1024
+T2, S2 = 2048, 1024
+FLOPS = 2 * (K1 + K2) * H * S + 2 * H * S2 * S
+
+F32 = mybir.dt.float32
+BF16 = mybir.dt.bfloat16
+I32 = mybir.dt.int32
+U32 = mybir.dt.uint32
+U16 = mybir.dt.uint16
+U8 = mybir.dt.uint8
+FP8X4 = mybir.dt.float8_e4m3fn_x4
+FP4X4 = mybir.dt.float4_e2m1fn_x4
+ACT = mybir.ActivationFunctionType
+
+P = 128
+PACK = 4
+NB = 512
+HALVES = S // NB
+GROUPS = H // (P * PACK)
+ITEM_CHUNK = 256
+QUADS = 4
+
+
+def tile_list_listed_click_probabilities_kernel(
+    tc, tab_words, tab_scales, offs, tab2_words, tab2_scales, offs2, w1, w4_words, w4_scales, b1, b2, out
+):
+    nc = tc.nc
+    with ExitStack() as ctx:
+        lists = ctx.enter_context(tc.tile_pool(name="lists", bufs=1))
+        keep = ctx.enter_context(tc.tile_pool(name="keep", bufs=1))
+        ring = ctx.enter_context(tc.tile_pool(name="ring", bufs=6))
+        psum = ctx.enter_context(tc.psum_pool(name="psum", bufs=1))
+
+        def sb(name, shape, dtype, tag=""):
+            return keep.tile(shape, dtype, name=name, tag=tag or name, align_bytes=64)
+
+        def bank(b, cols=NB):
+            return psum.tile([P, cols], F32, name="bank%d" % b)
+
+        users = lists.tile([P, S // 16], U16, name="users")
+        items = lists.tile([P, S2 // 16], U16, name="items")
+
+        us_win = sb("us_win", [P, 2, T // 4], I32, "slot_e")
+        w4s_raw = sb("w4s_raw", [P, 2, H // 4], I32, "slot_d")
+        is_win = sb("is_win", [P, T2 // 4], I32, "slot_f")
+        b2_rows = sb("b2_rows", [P, P], F32)
+        warm = sb("warm", [P, 2], F32, "slot_a")
+        nc.vector.memset(warm[:], 0.0)
+        nc.vector.memset(us_win[:, 0, :], 0)
+        nc.gpsimd.memset(us_win[:, 1, :], 0)
+        nc.scalar.activation(warm[:, 1:2], warm[:, 0:1], ACT.Sigmoid)
+        nc.vector.memset(w4s_raw[:], 0)
+        nc.vector.memset(is_win[:], 0)
+        nc.vector.memset(b2_rows[:], 0.0)
+
+        nc.sync.dma_start(users[:], offs)
+        nc.sync.dma_start(items[:], offs2)
+        b1_cols = sb("b1_cols", [P, GROUPS, PACK], F32)
+        nc.sync.dma_start(b1_cols[:], b1.rearrange("(g p t) -> p g t", p=P, t=PACK))
+        w4w_raw = sb("w4w_raw", [P, 2, 2 * H // 4], I32, "slot_b")
+        nc.sync.dma_start(w4w_raw[:], w4_words.rearrange("a p c -> p a c").bitcast(I32))
+        w1_rows = w1.rearrange("(p j) c -> p j c", j=PACK)
+        w1_raw = [sb("w1_raw0", [P, PACK, P * PACK], F32, "slot_c")]
+        nc.sync.dma_start(w1_raw[0][:], w1_rows[:, :, 0 : P * PACK])
+        for q in range(QUADS):
+            nc.sync.dma_start(
+                us_win[32 * q : 32 * q + 4, :, :],
+                tab_scales[1:3, 4 * q : 4 * q + 4, :].rearrange("a r t -> r a t").bitcast(I32),
+            )
+        uw_win = {}
+
+        def load_users(a, part, tag):
+            if part == 0:
+                uw_win[a] = sb("uw_win%d" % a, [P, T], I32, tag)
+            cols = slice(part * T // 2, (part + 1) * T // 2)
+            nc.sync.dma_start(uw_win[a][:, cols], tab_words[a].rearrange("p t i -> p (t i)").bitcast(I32)[:, cols])
+
+        def load_w4_scales(q):
+            nc.sync.dma_start(
+                w4s_raw[32 * q : 32 * q + 4, :, :],
+                w4_scales[:, 4 * q : 4 * q + 4, :].rearrange("a r t -> r a t").bitcast(I32),
+            )
+
+        def load_item_scales(q):
+            nc.sync.dma_start(
+                is_win[32 * q + 8 : 32 * q + 16, :],
+                tab2_scales[:, 4 * q : 4 * q + 4, :].bitcast(I32),
+            )
+
+        load_users(0, 0, "slot_a")
+        for q in range(QUADS):
+            nc.sync.dma_start(
+                us_win[32 * q + 4 : 32 * q + 8, 0, :],
+                tab_scales[0, 4 * q : 4 * q + 4, :].bitcast(I32),
+            )
+        load_users(0, 1, "slot_a")
+        load_w4_scales(0)
+        load_w4_scales(1)
+
+        w4w = sb("w4w", [P, 2 * 2 * H], U8)
+        w4s = sb("w4s", [P, 2 * H], U8)
+        nc.vector.tensor_copy(
+            w4w[:].bitcast(U16).rearrange("p (b t m) -> p b t m", t=PACK, m=P),
+            w4w_raw[:].rearrange("p a c -> p (a c)").bitcast(U16).rearrange("p (b m t) -> p b t m", t=PACK, m=P),
+        )
+        load_users(1, 0, "slot_b")
+        load_w4_scales(2)
+        load_w4_scales(3)
+        load_item_scales(0)
+        load_item_scales(1)
+        load_users(1, 1, "slot_b")
+        load_item_scales(2)
+        load_item_scales(3)
+        nc.sync.dma_start(b2_rows[0 : S2 // P, :], b2.rearrange("(i p) -> i p", p=P))
+
+        ident = sb("ident", [P, P], F32)
+        make_identity(nc, ident[:])
+        b2_ps = bank(7, P)
+        nc.tensor.transpose(b2_ps[:], b2_rows[:], ident[:])
+        b2_cols = sb("b2_cols", [P, S2 // P], F32)
+        nc.scalar.copy(b2_cols[:], b2_ps[:, 0 : S2 // P])
+
+        w1c = [sb("w1c%d" % g, [P, P * PACK], U32) for g in range(GROUPS)]
+        w1s = [sb("w1s%d" % g, [P, P * PACK], U8) for g in range(GROUPS)]
+        w1g = [sb("w1g%d" % g, [P, P * PACK * PACK], BF16, ("slot_g", "")[g]) for g in range(GROUPS)]
+
+        def w1_views(g):
+            return (
+                w1g[g][:].rearrange("p (t m j) -> p m t j", t=PACK, j=PACK),
+                w1_raw[g][:].rearrange("p j (m t) -> p m t j", t=PACK),
+            )
+
+        def w1_quantize(g):
+            nc.vector.quantize_mx(out=w1c[g][:].bitcast(FP8X4), scales=w1s[g][:], in_=w1g[g][:])
+
+        nc.scalar.copy(*w1_views(0))
+        load_users(2, 0, "slot_c")
+        load_users(2, 1, "slot_c")
+
+        def user_list(hf):
+            return users[:, hf * NB // 16 : (hf + 1) * NB // 16]
+
+        us = [[sb("us%d_%d" % (w, hf), [P, NB], U8) for hf in range(HALVES)] for w in range(2)]
+        for w in (1, 0):
+            for hf in range(HALVES):
+                nc.vector.tensor_copy(us[w][hf][:], us_win[:, w, :].bitcast(U8).indirect(user_list(hf)))
+        w1_quantize(0)
+        nc.vector.tensor_copy(
+            w4s[:].rearrange("p (b t m) -> p b t m", t=PACK, m=P),
+            w4s_raw[:].rearrange("p a c -> p (a c)").bitcast(U8).rearrange("p (b m t) -> p b t m", t=PACK, m=P),
+        )
+        w1_raw.append(sb("w1_raw1", [P, PACK, P * PACK], F32, "slot_g"))
+        nc.sync.dma_start(w1_raw[1][:], w1_rows[:, :, P * PACK : 2 * P * PACK])
+
+        uw = [[], [], []]
+
+        def gather_users(a, hf):
+            uw[a].append(sb("uw%d_%d" % (a, hf), [P, NB], U32, ("slot_e", "slot_d", "slot_f")[a] if hf == 0 else ""))
+            nc.vector.tensor_copy(uw[a][hf][:], uw_win[a][:].bitcast(U32).indirect(user_list(hf)))
+
+        def layer_pass(acc, g, t, hf, a, start, stop):
+            if a == 0:
+                cols = slice(t * P, (t + 1) * P)
+                lhsT, lhsT_scale = w1c[g][:, cols].bitcast(FP8X4), w1s[g][:, cols]
+                rhs_scale = us[0][hf][4:P, :]
+            else:
+                c0 = (a - 1) * H + (g * PACK + t) * P
+                lhsT, lhsT_scale = w4w[:, 2 * c0 : 2 * (c0 + P)].bitcast(FP4X4), w4s[:, c0 : c0 + P]
+                rhs_scale = us[a - 1][hf][:]
+            nc.tensor.matmul_mx(
+                out=acc[:], lhsT=lhsT, lhsT_scale=lhsT_scale,
+                rhs=uw[a][hf][:].bitcast(FP8X4), rhs_scale=rhs_scale, start=start, stop=stop,
+            )
+
+        hp = [[sb("hp%d_%d" % (g, hf), [P, PACK, NB], BF16) for hf in range(HALVES)] for g in range(GROUPS)]
+        hg = [[sb("hg%d_%d" % (g, hf), [P, NB * PACK], BF16) for hf in range(HALVES)] for g in range(GROUPS)]
+        hc = [[sb("hc%d_%d" % (g, hf), [P, NB], U32) for hf in range(HALVES)] for g in range(GROUPS)]
+        hs = [[sb("hs%d_%d" % (g, hf), [P, NB], U8) for hf in range(HALVES)] for g in range(GROUPS)]
+
+        def relu_out(acc, g, t, hf):
+            nc.scalar.activation(hp[g][hf][:, t, :], acc[:], ACT.Relu, bias=b1_cols[:, g, t : t + 1])
+
+        def quantize_h(g, hf):
+            w = NB // 2
+            for s in range(2):
+                nc.vector.tensor_copy(
+                    hg[g][hf][:, s * w * PACK : (s + 1) * w * PACK].rearrange("p (c i t) -> p c t i", i=4, t=PACK),
+                    hp[g][hf][:, :, s * w : (s + 1) * w].rearrange("p t (c i) -> p c t i", i=4),
+                )
+            for s in range(2):
+                nc.vector.quantize_mx(
+                    out=hc[g][hf][:, s * w : (s + 1) * w].bitcast(FP8X4),
+                    scales=hs[g][hf][:, s * w : (s + 1) * w],
+                    in_=hg[g][hf][:, s * w * PACK : (s + 1) * w * PACK],
+                )
+
+        isc = sb("isc", [P, S2], U8)
+
+        iw_win = []
+        accs = [[bank(PACK * hf + t) for t in range(PACK)] for hf in range(HALVES)]
+        for a in range(3):
+            for hf in range(HALVES):
+                gather_users(a, hf)
+                for t in range(PACK):
+                    layer_pass(accs[hf][t], 0, t, hf, a, a == 0, a == 2)
+                    if a == 2:
+                        relu_out(accs[hf][t], 0, t, hf)
+            if a < GROUPS:
+                iw_win.append(sb("iw_win%d" % a, [P, T2], I32, ("slot_a", "slot_b")[a]))
+                nc.sync.dma_start(iw_win[a][:], tab2_words[a].rearrange("p t i -> p (t i)").bitcast(I32))
+            if a == 1:
+                for s in range(4):
+                    nc.vector.tensor_copy(
+                        isc[:, s * 256 : (s + 1) * 256],
+                        is_win[:].bitcast(U8).indirect(items[:, s * 16 : (s + 1) * 16]),
+                    )
+
+        nc.vector.tensor_copy(*w1_views(1))
+        w1_quantize(1)
+
+        def layer_group1(hf):
+            group_accs = [bank(PACK * hf + t) for t in range(PACK)]
+            if hf == 0:
+                for t in range(PACK):
+                    for a in (1, 2):
+                        layer_pass(group_accs[t], 1, t, hf, a, a == 1, False)
+            for t in range(PACK):
+                if hf == 1:
+                    for a in (1, 2):
+                        layer_pass(group_accs[t], 1, t, hf, a, a == 1, False)
+                layer_pass(group_accs[t], 1, t, hf, 0, False, True)
+                relu_out(group_accs[t], 1, t, hf)
+
+        chunks = S2 // ITEM_CHUNK
+        iw = [[sb("iw%d_%d" % (a, c), [P, ITEM_CHUNK], U32) for c in range(chunks)] for a in range(GROUPS)]
+
+        def gather_items(c):
+            for a in range(GROUPS):
+                nc.vector.tensor_copy(
+                    iw[a][c][:],
+                    iw_win[a][:].bitcast(U32).indirect(items[:, c * ITEM_CHUNK // 16 : (c + 1) * ITEM_CHUNK // 16]),
+                )
+
+        def score(i, hf):
+            acc = bank(i)
+            c, within = divmod(i * P, ITEM_CHUNK)
+            for a in range(GROUPS):
+                nc.tensor.matmul_mx(
+                    out=acc[:],
+                    lhsT=iw[a][c][:, within : within + P].bitcast(FP8X4),
+                    lhsT_scale=isc[8 + 4 * a : P, i * P : (i + 1) * P],
+                    rhs=hc[a][hf][:].bitcast(FP8X4),
+                    rhs_scale=hs[a][hf][:],
+                    start=a == 0,
+                    stop=a == GROUPS - 1,
+                )
+            prob = ring.tile([P, NB], F32, name="prob")
+            nc.scalar.activation(prob[:], acc[:], ACT.Sigmoid, bias=b2_cols[:, i : i + 1])
+            nc.sync.dma_start(out[i * P : (i + 1) * P, hf * NB : (hf + 1) * NB], prob[:])
+
+        layer_group1(0)
+        quantize_h(0, 0)
+        layer_group1(1)
+        gather_items(0)
+        gather_items(1)
+        quantize_h(1, 0)
+        for i in range(S2 // P):
+            if i == 4:
+                gather_items(2)
+                quantize_h(0, 1)
+            if i == 6:
+                quantize_h(1, 1)
+                gather_items(3)
+            score(i, 0)
+        for i in range(S2 // P):
+            score(i, 1)

@@ -46,62 +46,58 @@ def tile_list_listed_click_probabilities_kernel(
         users = lists.tile([P, S // 16], U16, name="users")
         items = lists.tile([P, S2 // 16], U16, name="items")
 
-        us_win = sb("us_win", [P, 2, T // 4], I32, "slot_e")
+        us_win = sb("us_win", [P, T // 4], I32, "slot_e")
+        us_m = sb("us_m", [P, 2, S // 4], I32)
         w4s_raw = sb("w4s_raw", [P, 2, H // 4], I32, "slot_d")
         is_win = sb("is_win", [P, T2 // 4], I32, "slot_f")
+        is_m = sb("is_m", [P, S2 // 4], I32)
         b2_rows = sb("b2_rows", [P, P], F32)
         warm = sb("warm", [P, 2], F32, "slot_a")
         nc.vector.memset(warm[:], 0.0)
-        nc.vector.memset(us_win[:, 0, :], 0)
-        nc.gpsimd.memset(us_win[:, 1, :], 0)
+        nc.gpsimd.memset(b2_rows[:], 0.0)
+        nc.gpsimd.memset(us_win[:, 0 : T // 8], 0)
+        nc.vector.memset(us_win[:, T // 8 : T // 4], 0)
         nc.scalar.activation(warm[:, 1:2], warm[:, 0:1], ACT.Sigmoid)
         nc.vector.memset(w4s_raw[:], 0)
         nc.vector.memset(is_win[:], 0)
-        nc.vector.memset(b2_rows[:], 0.0)
+        nc.vector.memset(us_m[:], 0)
+        nc.vector.memset(is_m[:], 0)
 
         nc.sync.dma_start(users[:], offs)
         nc.sync.dma_start(items[:], offs2)
         b1_cols = sb("b1_cols", [P, GROUPS, PACK], F32)
         nc.sync.dma_start(b1_cols[:], b1.rearrange("(g p t) -> p g t", p=P, t=PACK))
-        w4w_raw = sb("w4w_raw", [P, 2, 2 * H // 4], I32, "slot_b")
+        nc.sync.dma_start(b2_rows[0 : S2 // P, :], b2.rearrange("(i p) -> i p", p=P))
+        nc.sync.dma_start(us_win[0:P:4, :], tab_scales[1:3].rearrange("a q t -> (a q) t").bitcast(I32))
+        nc.sync.dma_start(us_win[2:P:8, :], tab_scales[0].bitcast(I32))
+        w4w_raw = sb("w4w_raw", [P, 2, 2 * H // 4], I32)
         nc.sync.dma_start(w4w_raw[:], w4_words.rearrange("a p c -> p a c").bitcast(I32))
         w1_rows = w1.rearrange("(p j) c -> p j c", j=PACK)
         w1_raw = [sb("w1_raw0", [P, PACK, P * PACK], F32, "slot_c")]
         nc.sync.dma_start(w1_raw[0][:], w1_rows[:, :, 0 : P * PACK])
-        for q in range(QUADS):
-            nc.sync.dma_start(
-                us_win[32 * q : 32 * q + 4, :, :],
-                tab_scales[1:3, 4 * q : 4 * q + 4, :].rearrange("a r t -> r a t").bitcast(I32),
-            )
         uw_win = {}
 
-        def load_users(a, part, tag):
-            if part == 0:
-                uw_win[a] = sb("uw_win%d" % a, [P, T], I32, tag)
-            cols = slice(part * T // 2, (part + 1) * T // 2)
-            nc.sync.dma_start(uw_win[a][:, cols], tab_words[a].rearrange("p t i -> p (t i)").bitcast(I32)[:, cols])
+        def load_users(a, tag):
+            uw_win[a] = sb("uw_win%d" % a, [P, T], I32, tag)
+            nc.sync.dma_start(uw_win[a][:], tab_words[a].rearrange("p t i -> p (t i)").bitcast(I32))
 
-        def load_w4_scales(q):
+        for r in range(4):
             nc.sync.dma_start(
-                w4s_raw[32 * q : 32 * q + 4, :, :],
-                w4_scales[:, 4 * q : 4 * q + 4, :].rearrange("a r t -> r a t").bitcast(I32),
+                w4s_raw[r:P:32, :, :],
+                w4_scales[:, r:16:4, :].rearrange("a q c -> q a c").bitcast(I32),
             )
+        nc.sync.dma_start(is_win[0:P:4, :], tab2_scales.rearrange("a q t -> (a q) t").bitcast(I32))
+        load_users(0, "slot_a")
 
-        def load_item_scales(q):
-            nc.sync.dma_start(
-                is_win[32 * q + 8 : 32 * q + 16, :],
-                tab2_scales[:, 4 * q : 4 * q + 4, :].bitcast(I32),
-            )
-
-        load_users(0, 0, "slot_a")
-        for q in range(QUADS):
-            nc.sync.dma_start(
-                us_win[32 * q + 4 : 32 * q + 8, 0, :],
-                tab_scales[0, 4 * q : 4 * q + 4, :].bitcast(I32),
-            )
-        load_users(0, 1, "slot_a")
-        load_w4_scales(0)
-        load_w4_scales(1)
+        us_g = sb("us_g", [P, S // 4], I32)
+        nc.vector.tensor_copy(us_g[:].bitcast(U8), us_win[:].bitcast(U8).indirect(users[:]))
+        moves = [(us_m[4 + r : P : 32, 0, :], us_g[2 + 8 * r : P : 32, :]) for r in range(4)]
+        for a in (1, 2):
+            moves += [(us_m[r:P:32, a - 1, :], us_g[64 * (a - 1) + 4 * r : 64 * a : 16, :]) for r in range(4)]
+        for n, (dst, src) in enumerate(moves):
+            if n == 6:
+                load_users(1, "slot_e")
+            nc.sync.dma_start(dst, src)
 
         w4w = sb("w4w", [P, 2 * 2 * H], U8)
         w4s = sb("w4s", [P, 2 * H], U8)
@@ -109,15 +105,6 @@ def tile_list_listed_click_probabilities_kernel(
             w4w[:].bitcast(U16).rearrange("p (b t m) -> p b t m", t=PACK, m=P),
             w4w_raw[:].rearrange("p a c -> p (a c)").bitcast(U16).rearrange("p (b m t) -> p b t m", t=PACK, m=P),
         )
-        load_users(1, 0, "slot_b")
-        load_w4_scales(2)
-        load_w4_scales(3)
-        load_item_scales(0)
-        load_item_scales(1)
-        load_users(1, 1, "slot_b")
-        load_item_scales(2)
-        load_item_scales(3)
-        nc.sync.dma_start(b2_rows[0 : S2 // P, :], b2.rearrange("(i p) -> i p", p=P))
 
         ident = sb("ident", [P, P], F32)
         make_identity(nc, ident[:])
@@ -140,16 +127,13 @@ def tile_list_listed_click_probabilities_kernel(
             nc.vector.quantize_mx(out=w1c[g][:].bitcast(FP8X4), scales=w1s[g][:], in_=w1g[g][:])
 
         nc.scalar.copy(*w1_views(0))
-        load_users(2, 0, "slot_c")
-        load_users(2, 1, "slot_c")
+        load_users(2, "slot_c")
 
         def user_list(hf):
             return users[:, hf * NB // 16 : (hf + 1) * NB // 16]
 
-        us = [[sb("us%d_%d" % (w, hf), [P, NB], U8) for hf in range(HALVES)] for w in range(2)]
-        for w in (1, 0):
-            for hf in range(HALVES):
-                nc.vector.tensor_copy(us[w][hf][:], us_win[:, w, :].bitcast(U8).indirect(user_list(hf)))
+        is_g = sb("is_g", [P, S2 // 4], I32)
+        nc.vector.tensor_copy(is_g[:].bitcast(U8), is_win[:].bitcast(U8).indirect(items[:]))
         w1_quantize(0)
         nc.vector.tensor_copy(
             w4s[:].rearrange("p (b t m) -> p b t m", t=PACK, m=P),
@@ -161,18 +145,18 @@ def tile_list_listed_click_probabilities_kernel(
         uw = [[], [], []]
 
         def gather_users(a, hf):
-            uw[a].append(sb("uw%d_%d" % (a, hf), [P, NB], U32, ("slot_e", "slot_d", "slot_f")[a] if hf == 0 else ""))
+            uw[a].append(sb("uw%d_%d" % (a, hf), [P, NB], U32, ("", "slot_d", "slot_f")[a] if hf == 0 else ""))
             nc.vector.tensor_copy(uw[a][hf][:], uw_win[a][:].bitcast(U32).indirect(user_list(hf)))
 
         def layer_pass(acc, g, t, hf, a, start, stop):
             if a == 0:
                 cols = slice(t * P, (t + 1) * P)
                 lhsT, lhsT_scale = w1c[g][:, cols].bitcast(FP8X4), w1s[g][:, cols]
-                rhs_scale = us[0][hf][4:P, :]
+                rhs_scale = us_m[4:P, 0, :].bitcast(U8)[:, hf * NB : (hf + 1) * NB]
             else:
                 c0 = (a - 1) * H + (g * PACK + t) * P
                 lhsT, lhsT_scale = w4w[:, 2 * c0 : 2 * (c0 + P)].bitcast(FP4X4), w4s[:, c0 : c0 + P]
-                rhs_scale = us[a - 1][hf][:]
+                rhs_scale = us_m[:, a - 1, :].bitcast(U8)[:, hf * NB : (hf + 1) * NB]
             nc.tensor.matmul_mx(
                 out=acc[:], lhsT=lhsT, lhsT_scale=lhsT_scale,
                 rhs=uw[a][hf][:].bitcast(FP8X4), rhs_scale=rhs_scale, start=start, stop=stop,
@@ -200,7 +184,6 @@ def tile_list_listed_click_probabilities_kernel(
                     in_=hg[g][hf][:, s * w * PACK : (s + 1) * w * PACK],
                 )
 
-        isc = sb("isc", [P, S2], U8)
 
         iw_win = []
         accs = [[bank(PACK * hf + t) for t in range(PACK)] for hf in range(HALVES)]
@@ -212,14 +195,13 @@ def tile_list_listed_click_probabilities_kernel(
                     if a == 2:
                         relu_out(accs[hf][t], 0, t, hf)
             if a < GROUPS:
-                iw_win.append(sb("iw_win%d" % a, [P, T2], I32, ("slot_a", "slot_b")[a]))
+                iw_win.append(sb("iw_win%d" % a, [P, T2], I32, ("slot_a", "slot_e")[a]))
                 nc.sync.dma_start(iw_win[a][:], tab2_words[a].rearrange("p t i -> p (t i)").bitcast(I32))
             if a == 1:
-                for s in range(4):
-                    nc.vector.tensor_copy(
-                        isc[:, s * 256 : (s + 1) * 256],
-                        is_win[:].bitcast(U8).indirect(items[:, s * 16 : (s + 1) * 16]),
-                    )
+                for g in range(GROUPS):
+                    for r in range(4):
+                        first = 64 * g + 4 * r
+                        nc.sync.dma_start(is_m[8 + 4 * g + r : P : 32, :], is_g[first : 64 * (g + 1) : 16, :])
 
         nc.vector.tensor_copy(*w1_views(1))
         w1_quantize(1)
@@ -254,7 +236,7 @@ def tile_list_listed_click_probabilities_kernel(
                 nc.tensor.matmul_mx(
                     out=acc[:],
                     lhsT=iw[a][c][:, within : within + P].bitcast(FP8X4),
-                    lhsT_scale=isc[8 + 4 * a : P, i * P : (i + 1) * P],
+                    lhsT_scale=is_m[8 + 4 * a : P, :].bitcast(U8)[:, i * P : (i + 1) * P],
                     rhs=hc[a][hf][:].bitcast(FP8X4),
                     rhs_scale=hs[a][hf][:],
                     start=a == 0,

@@ -47,21 +47,17 @@ def tile_list_listed_click_probabilities_kernel(
         items = lists.tile([P, S2 // 16], U16, name="items")
 
         us_win = sb("us_win", [P, T // 4], I32, "slot_e")
-        us_m = sb("us_m", [P, 2, S // 4], I32)
+        us_m = [sb("us_m%d" % a, [P, S // 4], I32) for a in range(3)]
         w4s_raw = sb("w4s_raw", [P, 2, H // 4], I32, "slot_d")
         is_win = sb("is_win", [P, T2 // 4], I32, "slot_f")
-        is_m = sb("is_m", [P, S2 // 4], I32)
-        b2_rows = sb("b2_rows", [P, P], F32)
-        warm = sb("warm", [P, 2], F32, "slot_a")
-        nc.vector.memset(warm[:], 0.0)
+        b2_rows = sb("b2_rows", [P, P], F32, "slot_a")
         nc.gpsimd.memset(b2_rows[:], 0.0)
         nc.gpsimd.memset(us_win[:, 0 : T // 8], 0)
         nc.vector.memset(us_win[:, T // 8 : T // 4], 0)
-        nc.scalar.activation(warm[:, 1:2], warm[:, 0:1], ACT.Sigmoid)
         nc.vector.memset(w4s_raw[:], 0)
         nc.vector.memset(is_win[:], 0)
-        nc.vector.memset(us_m[:], 0)
-        nc.vector.memset(is_m[:], 0)
+        for a in range(3):
+            nc.vector.memset(us_m[a][:], 0)
 
         nc.sync.dma_start(users[:], offs)
         nc.sync.dma_start(items[:], offs2)
@@ -87,13 +83,20 @@ def tile_list_listed_click_probabilities_kernel(
                 w4_scales[:, r:16:4, :].rearrange("a q c -> q a c").bitcast(I32),
             )
         nc.sync.dma_start(is_win[0:P:4, :], tab2_scales.rearrange("a q t -> (a q) t").bitcast(I32))
+        ident = sb("ident", [P, P], F32)
+        make_identity(nc, ident[:])
+        b2_ps = bank(7, P)
+        nc.tensor.transpose(b2_ps[:], b2_rows[:], ident[:])
+        b2_cols = sb("b2_cols", [P, S2 // P], F32)
+        nc.scalar.copy(b2_cols[:], b2_ps[:, 0 : S2 // P])
+
         load_users(0, "slot_a")
 
         us_g = sb("us_g", [P, S // 4], I32)
         nc.vector.tensor_copy(us_g[:].bitcast(U8), us_win[:].bitcast(U8).indirect(users[:]))
-        moves = [(us_m[4 + r : P : 32, 0, :], us_g[2 + 8 * r : P : 32, :]) for r in range(4)]
+        moves = [(us_m[0][r:P:32, :], us_g[2 + 8 * r : P : 32, :]) for r in range(4)]
         for a in (1, 2):
-            moves += [(us_m[r:P:32, a - 1, :], us_g[64 * (a - 1) + 4 * r : 64 * a : 16, :]) for r in range(4)]
+            moves += [(us_m[a][r:P:32, :], us_g[64 * (a - 1) + 4 * r : 64 * a : 16, :]) for r in range(4)]
         for n, (dst, src) in enumerate(moves):
             if n == 6:
                 load_users(1, "slot_e")
@@ -105,13 +108,6 @@ def tile_list_listed_click_probabilities_kernel(
             w4w[:].bitcast(U16).rearrange("p (b t m) -> p b t m", t=PACK, m=P),
             w4w_raw[:].rearrange("p a c -> p (a c)").bitcast(U16).rearrange("p (b m t) -> p b t m", t=PACK, m=P),
         )
-
-        ident = sb("ident", [P, P], F32)
-        make_identity(nc, ident[:])
-        b2_ps = bank(7, P)
-        nc.tensor.transpose(b2_ps[:], b2_rows[:], ident[:])
-        b2_cols = sb("b2_cols", [P, S2 // P], F32)
-        nc.scalar.copy(b2_cols[:], b2_ps[:, 0 : S2 // P])
 
         w1c = [sb("w1c%d" % g, [P, P * PACK], U32) for g in range(GROUPS)]
         w1s = [sb("w1s%d" % g, [P, P * PACK], U8) for g in range(GROUPS)]
@@ -133,12 +129,7 @@ def tile_list_listed_click_probabilities_kernel(
             return users[:, hf * NB // 16 : (hf + 1) * NB // 16]
 
         is_g = sb("is_g", [P, S2 // 4], I32)
-        nc.vector.tensor_copy(is_g[:].bitcast(U8), is_win[:].bitcast(U8).indirect(items[:]))
         w1_quantize(0)
-        nc.vector.tensor_copy(
-            w4s[:].rearrange("p (b t m) -> p b t m", t=PACK, m=P),
-            w4s_raw[:].rearrange("p a c -> p (a c)").bitcast(U8).rearrange("p (b m t) -> p b t m", t=PACK, m=P),
-        )
         w1_raw.append(sb("w1_raw1", [P, PACK, P * PACK], F32, "slot_g"))
         nc.sync.dma_start(w1_raw[1][:], w1_rows[:, :, P * PACK : 2 * P * PACK])
 
@@ -152,18 +143,18 @@ def tile_list_listed_click_probabilities_kernel(
             if a == 0:
                 cols = slice(t * P, (t + 1) * P)
                 lhsT, lhsT_scale = w1c[g][:, cols].bitcast(FP8X4), w1s[g][:, cols]
-                rhs_scale = us_m[4:P, 0, :].bitcast(U8)[:, hf * NB : (hf + 1) * NB]
+                rhs_scale = us_m[0][:].bitcast(U8)[:, hf * NB : (hf + 1) * NB]
             else:
                 c0 = (a - 1) * H + (g * PACK + t) * P
                 lhsT, lhsT_scale = w4w[:, 2 * c0 : 2 * (c0 + P)].bitcast(FP4X4), w4s[:, c0 : c0 + P]
-                rhs_scale = us_m[:, a - 1, :].bitcast(U8)[:, hf * NB : (hf + 1) * NB]
+                rhs_scale = us_m[a][:].bitcast(U8)[:, hf * NB : (hf + 1) * NB]
             nc.tensor.matmul_mx(
                 out=acc[:], lhsT=lhsT, lhsT_scale=lhsT_scale,
                 rhs=uw[a][hf][:].bitcast(FP8X4), rhs_scale=rhs_scale, start=start, stop=stop,
             )
 
-        hp = [[sb("hp%d_%d" % (g, hf), [P, PACK, NB], BF16) for hf in range(HALVES)] for g in range(GROUPS)]
-        hg = [[sb("hg%d_%d" % (g, hf), [P, NB * PACK], BF16) for hf in range(HALVES)] for g in range(GROUPS)]
+        hp = [[sb("hp%d_%d" % (g, hf), [P, PACK, NB], BF16, "slot_h" if g + hf == 0 else "") for hf in range(HALVES)] for g in range(GROUPS)]
+        hg = [[sb("hg%d_%d" % (g, hf), [P, NB * PACK], BF16, "slot_i" if g + hf == 0 else "") for hf in range(HALVES)] for g in range(GROUPS)]
         hc = [[sb("hc%d_%d" % (g, hf), [P, NB], U32) for hf in range(HALVES)] for g in range(GROUPS)]
         hs = [[sb("hs%d_%d" % (g, hf), [P, NB], U8) for hf in range(HALVES)] for g in range(GROUPS)]
 
@@ -194,16 +185,26 @@ def tile_list_listed_click_probabilities_kernel(
                     layer_pass(accs[hf][t], 0, t, hf, a, a == 0, a == 2)
                     if a == 2:
                         relu_out(accs[hf][t], 0, t, hf)
+            if a == 0:
+                nc.vector.tensor_copy(
+                    w4s[:].rearrange("p (b t m) -> p b t m", t=PACK, m=P),
+                    w4s_raw[:].rearrange("p a c -> p (a c)").bitcast(U8).rearrange("p (b m t) -> p b t m", t=PACK, m=P),
+                )
+                for s in range(2):
+                    nc.vector.tensor_copy(
+                        is_g[:].bitcast(U8)[:, s * 512 : (s + 1) * 512],
+                        is_win[:].bitcast(U8).indirect(items[:, s * 32 : (s + 1) * 32]),
+                    )
             if a < GROUPS:
                 iw_win.append(sb("iw_win%d" % a, [P, T2], I32, ("slot_a", "slot_e")[a]))
                 nc.sync.dma_start(iw_win[a][:], tab2_words[a].rearrange("p t i -> p (t i)").bitcast(I32))
-            if a == 1:
-                for g in range(GROUPS):
-                    for r in range(4):
-                        first = 64 * g + 4 * r
-                        nc.sync.dma_start(is_m[8 + 4 * g + r : P : 32, :], is_g[first : 64 * (g + 1) : 16, :])
 
         nc.vector.tensor_copy(*w1_views(1))
+        is_m = sb("is_m", [P, S2 // 4], I32, "slot_c")
+        nc.vector.memset(is_m[:], 0)
+        for g in range(GROUPS):
+            for r in range(4):
+                nc.sync.dma_start(is_m[8 + 4 * g + r : P : 32, :], is_g[64 * g + 4 * r : 64 * (g + 1) : 16, :])
         w1_quantize(1)
 
         def layer_group1(hf):
@@ -219,23 +220,21 @@ def tile_list_listed_click_probabilities_kernel(
                 layer_pass(group_accs[t], 1, t, hf, 0, False, True)
                 relu_out(group_accs[t], 1, t, hf)
 
-        chunks = S2 // ITEM_CHUNK
-        iw = [[sb("iw%d_%d" % (a, c), [P, ITEM_CHUNK], U32) for c in range(chunks)] for a in range(GROUPS)]
+        iw = []
 
         def gather_items(c):
             for a in range(GROUPS):
                 nc.vector.tensor_copy(
-                    iw[a][c][:],
+                    iw[a][:, c * ITEM_CHUNK : (c + 1) * ITEM_CHUNK],
                     iw_win[a][:].bitcast(U32).indirect(items[:, c * ITEM_CHUNK // 16 : (c + 1) * ITEM_CHUNK // 16]),
                 )
 
         def score(i, hf):
             acc = bank(i)
-            c, within = divmod(i * P, ITEM_CHUNK)
             for a in range(GROUPS):
                 nc.tensor.matmul_mx(
                     out=acc[:],
-                    lhsT=iw[a][c][:, within : within + P].bitcast(FP8X4),
+                    lhsT=iw[a][:, i * P : (i + 1) * P].bitcast(FP8X4),
                     lhsT_scale=is_m[8 + 4 * a : P, :].bitcast(U8)[:, i * P : (i + 1) * P],
                     rhs=hc[a][hf][:].bitcast(FP8X4),
                     rhs_scale=hs[a][hf][:],
@@ -243,11 +242,15 @@ def tile_list_listed_click_probabilities_kernel(
                     stop=a == GROUPS - 1,
                 )
             prob = ring.tile([P, NB], F32, name="prob")
-            nc.scalar.activation(prob[:], acc[:], ACT.Sigmoid, bias=b2_cols[:, i : i + 1])
-            nc.sync.dma_start(out[i * P : (i + 1) * P, hf * NB : (hf + 1) * NB], prob[:])
+            pieces = 2 if (i, hf) == (S2 // P - 1, HALVES - 1) else 1
+            for s in range(pieces):
+                cols = slice(s * NB // pieces, (s + 1) * NB // pieces)
+                nc.scalar.activation(prob[:, cols], acc[:, cols], ACT.Sigmoid, bias=b2_cols[:, i : i + 1])
+                nc.sync.dma_start(out[i * P : (i + 1) * P, hf * NB : (hf + 1) * NB][:, cols], prob[:, cols])
 
         layer_group1(0)
         quantize_h(0, 0)
+        iw += [sb("iw%d" % a, [P, S2], U32, ("slot_h", "slot_i")[a]) for a in range(GROUPS)]
         layer_group1(1)
         gather_items(0)
         gather_items(1)

@@ -20,11 +20,22 @@ ACT = mybir.ActivationFunctionType
 
 P = 128
 PACK = 4
-NB = 512
-HALVES = S // NB
-GROUPS = H // (P * PACK)
-ITEM_CHUNK = 256
-QUADS = 4
+K_PASS = P * PACK
+QUAD = 32
+ROWS = 4
+BYTES = 4
+PER_COLUMN = 16
+BANK = 512
+BANKS = 8
+HALVES = S // BANK
+USER_PASSES = (K1 + K2) // K_PASS
+W4_PASSES = K2 // K_PASS
+GROUPS = H // K_PASS
+ITEM_TILES = S2 // P
+ITEM_CHUNK = 2 * P
+ITEM_SHIFT = 8
+MOVES_AHEAD = 6
+PIECES = 2
 
 
 def tile_list_listed_click_probabilities_kernel(
@@ -34,234 +45,252 @@ def tile_list_listed_click_probabilities_kernel(
     with ExitStack() as ctx:
         lists = ctx.enter_context(tc.tile_pool(name="lists", bufs=1))
         keep = ctx.enter_context(tc.tile_pool(name="keep", bufs=1))
-        ring = ctx.enter_context(tc.tile_pool(name="ring", bufs=6))
+        results = ctx.enter_context(tc.tile_pool(name="results", bufs=ITEM_TILES * HALVES))
         psum = ctx.enter_context(tc.psum_pool(name="psum", bufs=1))
 
-        def sb(name, shape, dtype, tag=""):
+        def sbuf(name, shape, dtype, tag=None):
             return keep.tile(shape, dtype, name=name, tag=tag or name, align_bytes=64)
 
-        def bank(b, cols=NB):
-            return psum.tile([P, cols], F32, name="bank%d" % b)
+        def bank(b, columns=BANK):
+            return psum.tile([P, columns], F32, name="bank%d" % b)
 
-        users = lists.tile([P, S // 16], U16, name="users")
-        items = lists.tile([P, S2 // 16], U16, name="items")
+        def entries(listed, first, count):
+            return listed[:, first // PER_COLUMN : (first + count) // PER_COLUMN]
 
-        us_win = sb("us_win", [P, T // 4], I32, "slot_e")
-        us_m = [sb("us_m%d" % a, [P, S // 4], I32) for a in range(3)]
-        w4s_raw = sb("w4s_raw", [P, 2, H // 4], I32, "slot_d")
-        is_win = sb("is_win", [P, T2 // 4], I32, "slot_f")
-        b2_rows = sb("b2_rows", [P, P], F32, "slot_a")
+        users = lists.tile([P, S // PER_COLUMN], U16, name="users")
+        items = lists.tile([P, S2 // PER_COLUMN], U16, name="items")
+
+        user_rows = sbuf("user_rows", [P, T // BYTES], I32, "shared_e")
+        user_plane = [sbuf("user_plane%d" % a, [P, S // BYTES], I32) for a in range(USER_PASSES)]
+        w4_plane_raw = sbuf("w4_plane_raw", [P, W4_PASSES, H // BYTES], I32, "shared_d")
+        item_rows = sbuf("item_rows", [P, T2 // BYTES], I32, "shared_f")
+        b2_rows = sbuf("b2_rows", [P, P], F32, "shared_a")
+        middle = T // BYTES // 2
         nc.gpsimd.memset(b2_rows[:], 0.0)
-        nc.gpsimd.memset(us_win[:, 0 : T // 8], 0)
-        nc.vector.memset(us_win[:, T // 8 : T // 4], 0)
-        nc.vector.memset(w4s_raw[:], 0)
-        nc.vector.memset(is_win[:], 0)
-        for a in range(3):
-            nc.vector.memset(us_m[a][:], 0)
+        nc.gpsimd.memset(user_rows[:, :middle], 0)
+        nc.vector.memset(user_rows[:, middle:], 0)
+        nc.vector.memset(w4_plane_raw[:], 0)
+        nc.vector.memset(item_rows[:], 0)
+        for a in range(USER_PASSES):
+            nc.vector.memset(user_plane[a][:], 0)
 
+        w4_raw = sbuf("w4_raw", [P, W4_PASSES, 2 * H // BYTES], I32)
+        nc.sync.dma_start(w4_raw[:], w4_words.rearrange("a p c -> p a c").bitcast(I32))
         nc.sync.dma_start(users[:], offs)
         nc.sync.dma_start(items[:], offs2)
-        b1_cols = sb("b1_cols", [P, GROUPS, PACK], F32)
+        b1_cols = sbuf("b1_cols", [P, GROUPS, PACK], F32)
         nc.sync.dma_start(b1_cols[:], b1.rearrange("(g p t) -> p g t", p=P, t=PACK))
-        nc.sync.dma_start(b2_rows[0 : S2 // P, :], b2.rearrange("(i p) -> i p", p=P))
-        nc.sync.dma_start(us_win[0:P:4, :], tab_scales[1:3].rearrange("a q t -> (a q) t").bitcast(I32))
-        nc.sync.dma_start(us_win[2:P:8, :], tab_scales[0].bitcast(I32))
-        w4w_raw = sb("w4w_raw", [P, 2, 2 * H // 4], I32)
-        nc.sync.dma_start(w4w_raw[:], w4_words.rearrange("a p c -> p a c").bitcast(I32))
+        nc.sync.dma_start(b2_rows[0:ITEM_TILES, :], b2.rearrange("(i p) -> i p", p=P))
+        nc.sync.dma_start(user_rows[0:P:4, :], tab_scales[1:3].rearrange("a q t -> (a q) t").bitcast(I32))
+        nc.sync.dma_start(user_rows[2:P:8, :], tab_scales[0].bitcast(I32))
         w1_rows = w1.rearrange("(p j) c -> p j c", j=PACK)
-        w1_raw = [sb("w1_raw0", [P, PACK, P * PACK], F32, "slot_c")]
-        nc.sync.dma_start(w1_raw[0][:], w1_rows[:, :, 0 : P * PACK])
-        uw_win = {}
-
-        def load_users(a, tag):
-            uw_win[a] = sb("uw_win%d" % a, [P, T], I32, tag)
-            nc.sync.dma_start(uw_win[a][:], tab_words[a].rearrange("p t i -> p (t i)").bitcast(I32))
-
-        for r in range(4):
+        w1_raw = [sbuf("w1_raw0", [P, PACK, K_PASS], F32, "shared_c")]
+        nc.sync.dma_start(w1_raw[0][:], w1_rows[:, :, 0:K_PASS])
+        for r in range(ROWS):
             nc.sync.dma_start(
-                w4s_raw[r:P:32, :, :],
-                w4_scales[:, r:16:4, :].rearrange("a q c -> q a c").bitcast(I32),
+                w4_plane_raw[r:P:QUAD, :, :],
+                w4_scales[:, r : P // 8 : ROWS, :].rearrange("a q c -> q a c").bitcast(I32),
             )
-        nc.sync.dma_start(is_win[0:P:4, :], tab2_scales.rearrange("a q t -> (a q) t").bitcast(I32))
-        ident = sb("ident", [P, P], F32)
-        make_identity(nc, ident[:])
-        b2_ps = bank(7, P)
-        nc.tensor.transpose(b2_ps[:], b2_rows[:], ident[:])
-        b2_cols = sb("b2_cols", [P, S2 // P], F32)
-        nc.scalar.copy(b2_cols[:], b2_ps[:, 0 : S2 // P])
+        nc.sync.dma_start(item_rows[0:P:4, :], tab2_scales.rearrange("a q t -> (a q) t").bitcast(I32))
 
-        load_users(0, "slot_a")
+        identity = sbuf("identity", [P, P], F32)
+        make_identity(nc, identity[:])
+        b2_turned = bank(BANKS - 1, P)
+        nc.tensor.transpose(b2_turned[:], b2_rows[:], identity[:])
+        b2_cols = sbuf("b2_cols", [P, ITEM_TILES], F32)
+        nc.scalar.copy(b2_cols[:], b2_turned[:, 0:ITEM_TILES])
 
-        us_g = sb("us_g", [P, S // 4], I32)
-        nc.vector.tensor_copy(us_g[:].bitcast(U8), us_win[:].bitcast(U8).indirect(users[:]))
-        moves = [(us_m[0][r:P:32, :], us_g[2 + 8 * r : P : 32, :]) for r in range(4)]
-        for a in (1, 2):
-            moves += [(us_m[a][r:P:32, :], us_g[64 * (a - 1) + 4 * r : 64 * a : 16, :]) for r in range(4)]
-        for n, (dst, src) in enumerate(moves):
-            if n == 6:
-                load_users(1, "slot_e")
-            nc.sync.dma_start(dst, src)
+        user_table = []
 
-        w4w = sb("w4w", [P, 2 * 2 * H], U8)
-        w4s = sb("w4s", [P, 2 * H], U8)
-        nc.vector.tensor_copy(
-            w4w[:].bitcast(U16).rearrange("p (b t m) -> p b t m", t=PACK, m=P),
-            w4w_raw[:].rearrange("p a c -> p (a c)").bitcast(U16).rearrange("p (b m t) -> p b t m", t=PACK, m=P),
-        )
+        def load_user_pass(a, tag):
+            user_table.append(sbuf("user_table%d" % a, [P, T], I32, tag))
+            nc.sync.dma_start(user_table[a][:], tab_words[a].rearrange("p t i -> p (t i)").bitcast(I32))
 
-        w1c = [sb("w1c%d" % g, [P, P * PACK], U32) for g in range(GROUPS)]
-        w1s = [sb("w1s%d" % g, [P, P * PACK], U8) for g in range(GROUPS)]
-        w1g = [sb("w1g%d" % g, [P, P * PACK * PACK], BF16, ("slot_g", "")[g]) for g in range(GROUPS)]
+        load_user_pass(0, "shared_a")
 
-        def w1_views(g):
-            return (
-                w1g[g][:].rearrange("p (t m j) -> p m t j", t=PACK, j=PACK),
+        user_picked = sbuf("user_picked", [P, S // BYTES], I32)
+        nc.vector.tensor_copy(user_picked[:].bitcast(U8), user_rows[:].bitcast(U8).indirect(users[:]))
+        moves = [(user_plane[0][r:P:QUAD, :], user_picked[2 + 8 * r : P : 32, :]) for r in range(ROWS)]
+        for a in range(1, USER_PASSES):
+            moves += [(user_plane[a][r:P:QUAD, :], user_picked[64 * (a - 1) + 4 * r : 64 * a : 16, :]) for r in range(ROWS)]
+        for destination, source in moves[:MOVES_AHEAD]:
+            nc.sync.dma_start(destination, source)
+        load_user_pass(1, "shared_e")
+        for destination, source in moves[MOVES_AHEAD:]:
+            nc.sync.dma_start(destination, source)
+
+        def reorder_columns(ordered, raw):
+            nc.vector.tensor_copy(
+                ordered.rearrange("p (b t m) -> p b t m", t=PACK, m=P),
+                raw.rearrange("p (b m t) -> p b t m", t=PACK, m=P),
+            )
+
+        w4_codes = sbuf("w4_codes", [P, W4_PASSES * 2 * H], U8)
+        w4_plane = sbuf("w4_plane", [P, W4_PASSES * H], U8)
+        reorder_columns(w4_codes[:].bitcast(U16), w4_raw[:].rearrange("p a c -> p (a c)").bitcast(U16))
+
+        w1_codes = [sbuf("w1_codes%d" % g, [P, K_PASS], U32) for g in range(GROUPS)]
+        w1_plane = [sbuf("w1_plane%d" % g, [P, K_PASS], U8) for g in range(GROUPS)]
+        w1_bf16 = [sbuf("w1_bf16_0", [P, K_PASS * PACK], BF16, "shared_g"), sbuf("w1_bf16_1", [P, K_PASS * PACK], BF16)]
+
+        def round_w1(g, copy):
+            copy(
+                w1_bf16[g][:].rearrange("p (t m j) -> p m t j", t=PACK, j=PACK),
                 w1_raw[g][:].rearrange("p j (m t) -> p m t j", t=PACK),
             )
 
-        def w1_quantize(g):
-            nc.vector.quantize_mx(out=w1c[g][:].bitcast(FP8X4), scales=w1s[g][:], in_=w1g[g][:])
+        def quantize_w1(g):
+            nc.vector.quantize_mx(out=w1_codes[g][:].bitcast(FP8X4), scales=w1_plane[g][:], in_=w1_bf16[g][:])
 
-        nc.scalar.copy(*w1_views(0))
-        load_users(2, "slot_c")
+        round_w1(0, nc.scalar.copy)
+        load_user_pass(2, "shared_c")
+        item_picked = sbuf("item_picked", [P, S2 // BYTES], I32)
+        quantize_w1(0)
+        w1_raw.append(sbuf("w1_raw1", [P, PACK, K_PASS], F32, "shared_g"))
+        nc.sync.dma_start(w1_raw[1][:], w1_rows[:, :, K_PASS : 2 * K_PASS])
 
-        def user_list(hf):
-            return users[:, hf * NB // 16 : (hf + 1) * NB // 16]
+        user_words = {}
+        user_words_tag = {(1, 0): "shared_d", (2, 0): "shared_f"}
 
-        is_g = sb("is_g", [P, S2 // 4], I32)
-        w1_quantize(0)
-        w1_raw.append(sb("w1_raw1", [P, PACK, P * PACK], F32, "slot_g"))
-        nc.sync.dma_start(w1_raw[1][:], w1_rows[:, :, P * PACK : 2 * P * PACK])
+        def gather_users(a, half):
+            user_words[a, half] = sbuf("user_words%d_%d" % (a, half), [P, BANK], U32, user_words_tag.get((a, half)))
+            window = user_table[a][:].bitcast(U32)
+            nc.vector.tensor_copy(user_words[a, half][:], window.indirect(entries(users, half * BANK, BANK)))
 
-        uw = [[], [], []]
-
-        def gather_users(a, hf):
-            uw[a].append(sb("uw%d_%d" % (a, hf), [P, NB], U32, ("", "slot_d", "slot_f")[a] if hf == 0 else ""))
-            nc.vector.tensor_copy(uw[a][hf][:], uw_win[a][:].bitcast(U32).indirect(user_list(hf)))
-
-        def layer_pass(acc, g, t, hf, a, start, stop):
+        def layer_pass(acc, g, t, half, a, start, stop):
             if a == 0:
-                cols = slice(t * P, (t + 1) * P)
-                lhsT, lhsT_scale = w1c[g][:, cols].bitcast(FP8X4), w1s[g][:, cols]
-                rhs_scale = us_m[0][:].bitcast(U8)[:, hf * NB : (hf + 1) * NB]
+                columns = slice(t * P, (t + 1) * P)
+                weights, weight_scales = w1_codes[g][:, columns].bitcast(FP8X4), w1_plane[g][:, columns]
             else:
-                c0 = (a - 1) * H + (g * PACK + t) * P
-                lhsT, lhsT_scale = w4w[:, 2 * c0 : 2 * (c0 + P)].bitcast(FP4X4), w4s[:, c0 : c0 + P]
-                rhs_scale = us_m[a][:].bitcast(U8)[:, hf * NB : (hf + 1) * NB]
+                first = (a - 1) * H + (g * PACK + t) * P
+                weights = w4_codes[:, 2 * first : 2 * (first + P)].bitcast(FP4X4)
+                weight_scales = w4_plane[:, first : first + P]
             nc.tensor.matmul_mx(
-                out=acc[:], lhsT=lhsT, lhsT_scale=lhsT_scale,
-                rhs=uw[a][hf][:].bitcast(FP8X4), rhs_scale=rhs_scale, start=start, stop=stop,
+                out=acc[:],
+                lhsT=weights,
+                lhsT_scale=weight_scales,
+                rhs=user_words[a, half][:].bitcast(FP8X4),
+                rhs_scale=user_plane[a][:].bitcast(U8)[:, half * BANK : (half + 1) * BANK],
+                start=start,
+                stop=stop,
             )
 
-        hp = [[sb("hp%d_%d" % (g, hf), [P, PACK, NB], BF16, "slot_h" if g + hf == 0 else "") for hf in range(HALVES)] for g in range(GROUPS)]
-        hg = [[sb("hg%d_%d" % (g, hf), [P, NB * PACK], BF16, "slot_i" if g + hf == 0 else "") for hf in range(HALVES)] for g in range(GROUPS)]
-        hc = [[sb("hc%d_%d" % (g, hf), [P, NB], U32) for hf in range(HALVES)] for g in range(GROUPS)]
-        hs = [[sb("hs%d_%d" % (g, hf), [P, NB], U8) for hf in range(HALVES)] for g in range(GROUPS)]
+        blocks = [(g, half) for g in range(GROUPS) for half in range(HALVES)]
+        h_tiles = {b: sbuf("h_tiles%d_%d" % b, [P, PACK, BANK], BF16, "shared_h" if b == (0, 0) else None) for b in blocks}
+        h_packed = {b: sbuf("h_packed%d_%d" % b, [P, BANK * PACK], BF16, "shared_i" if b == (0, 0) else None) for b in blocks}
+        h_codes = {b: sbuf("h_codes%d_%d" % b, [P, BANK], U32) for b in blocks}
+        h_plane = {b: sbuf("h_plane%d_%d" % b, [P, BANK], U8) for b in blocks}
 
-        def relu_out(acc, g, t, hf):
-            nc.scalar.activation(hp[g][hf][:, t, :], acc[:], ACT.Relu, bias=b1_cols[:, g, t : t + 1])
+        def relu_out(acc, g, t, half):
+            nc.scalar.activation(h_tiles[g, half][:, t, :], acc[:], ACT.Relu, bias=b1_cols[:, g, t : t + 1])
 
-        def quantize_h(g, hf):
-            w = NB // 2
-            for s in range(2):
+        def quantize_h(g, half):
+            width = BANK // PIECES
+            for s in range(PIECES):
                 nc.vector.tensor_copy(
-                    hg[g][hf][:, s * w * PACK : (s + 1) * w * PACK].rearrange("p (c i t) -> p c t i", i=4, t=PACK),
-                    hp[g][hf][:, :, s * w : (s + 1) * w].rearrange("p t (c i) -> p c t i", i=4),
+                    h_packed[g, half][:, s * width * PACK : (s + 1) * width * PACK].rearrange(
+                        "p (c i t) -> p c t i", i=4, t=PACK
+                    ),
+                    h_tiles[g, half][:, :, s * width : (s + 1) * width].rearrange("p t (c i) -> p c t i", i=4),
                 )
-            for s in range(2):
+            for s in range(PIECES):
                 nc.vector.quantize_mx(
-                    out=hc[g][hf][:, s * w : (s + 1) * w].bitcast(FP8X4),
-                    scales=hs[g][hf][:, s * w : (s + 1) * w],
-                    in_=hg[g][hf][:, s * w * PACK : (s + 1) * w * PACK],
+                    out=h_codes[g, half][:, s * width : (s + 1) * width].bitcast(FP8X4),
+                    scales=h_plane[g, half][:, s * width : (s + 1) * width],
+                    in_=h_packed[g, half][:, s * width * PACK : (s + 1) * width * PACK],
                 )
 
-
-        iw_win = []
-        accs = [[bank(PACK * hf + t) for t in range(PACK)] for hf in range(HALVES)]
-        for a in range(3):
-            for hf in range(HALVES):
-                gather_users(a, hf)
+        item_table = []
+        group0 = [[bank(PACK * half + t) for t in range(PACK)] for half in range(HALVES)]
+        last_pass = USER_PASSES - 1
+        for a in range(USER_PASSES):
+            for half in range(HALVES):
+                gather_users(a, half)
                 for t in range(PACK):
-                    layer_pass(accs[hf][t], 0, t, hf, a, a == 0, a == 2)
-                    if a == 2:
-                        relu_out(accs[hf][t], 0, t, hf)
+                    layer_pass(group0[half][t], 0, t, half, a, a == 0, a == last_pass)
+                    if a == last_pass:
+                        relu_out(group0[half][t], 0, t, half)
             if a == 0:
-                nc.vector.tensor_copy(
-                    w4s[:].rearrange("p (b t m) -> p b t m", t=PACK, m=P),
-                    w4s_raw[:].rearrange("p a c -> p (a c)").bitcast(U8).rearrange("p (b m t) -> p b t m", t=PACK, m=P),
-                )
-                for s in range(2):
+                reorder_columns(w4_plane[:], w4_plane_raw[:].rearrange("p a c -> p (a c)").bitcast(U8))
+                for first in (0, S2 // 2):
                     nc.vector.tensor_copy(
-                        is_g[:].bitcast(U8)[:, s * 512 : (s + 1) * 512],
-                        is_win[:].bitcast(U8).indirect(items[:, s * 32 : (s + 1) * 32]),
+                        item_picked[:].bitcast(U8)[:, first : first + S2 // 2],
+                        item_rows[:].bitcast(U8).indirect(entries(items, first, S2 // 2)),
                     )
             if a < GROUPS:
-                iw_win.append(sb("iw_win%d" % a, [P, T2], I32, ("slot_a", "slot_e")[a]))
-                nc.sync.dma_start(iw_win[a][:], tab2_words[a].rearrange("p t i -> p (t i)").bitcast(I32))
+                item_table.append(sbuf("item_table%d" % a, [P, T2], I32, ("shared_a", "shared_e")[a]))
+                nc.sync.dma_start(item_table[a][:], tab2_words[a].rearrange("p t i -> p (t i)").bitcast(I32))
 
-        nc.vector.tensor_copy(*w1_views(1))
-        is_m = sb("is_m", [P, S2 // 4], I32, "slot_c")
-        nc.vector.memset(is_m[:], 0)
+        round_w1(1, nc.vector.tensor_copy)
+        item_plane = sbuf("item_plane", [P, S2 // BYTES], I32, "shared_c")
+        nc.vector.memset(item_plane[:], 0)
         for g in range(GROUPS):
-            for r in range(4):
-                nc.sync.dma_start(is_m[8 + 4 * g + r : P : 32, :], is_g[64 * g + 4 * r : 64 * (g + 1) : 16, :])
-        w1_quantize(1)
+            for r in range(ROWS):
+                nc.sync.dma_start(
+                    item_plane[ITEM_SHIFT + ROWS * g + r : P : QUAD, :],
+                    item_picked[64 * g + 4 * r : 64 * (g + 1) : 16, :],
+                )
+        quantize_w1(1)
 
-        def layer_group1(hf):
-            group_accs = [bank(PACK * hf + t) for t in range(PACK)]
-            if hf == 0:
-                for t in range(PACK):
-                    for a in (1, 2):
-                        layer_pass(group_accs[t], 1, t, hf, a, a == 1, False)
-            for t in range(PACK):
-                if hf == 1:
-                    for a in (1, 2):
-                        layer_pass(group_accs[t], 1, t, hf, a, a == 1, False)
-                layer_pass(group_accs[t], 1, t, hf, 0, False, True)
-                relu_out(group_accs[t], 1, t, hf)
+        def open_group1(acc, t, half):
+            for a in range(1, USER_PASSES):
+                layer_pass(acc, 1, t, half, a, a == 1, False)
 
-        iw = []
+        def close_group1(acc, t, half):
+            layer_pass(acc, 1, t, half, 0, False, True)
+            relu_out(acc, 1, t, half)
 
-        def gather_items(c):
-            for a in range(GROUPS):
+        sums = [bank(t) for t in range(PACK)]
+        for t in range(PACK):
+            open_group1(sums[t], t, 0)
+        for t in range(PACK):
+            close_group1(sums[t], t, 0)
+        quantize_h(0, 0)
+        item_words = [sbuf("item_words%d" % g, [P, S2], U32, ("shared_h", "shared_i")[g]) for g in range(GROUPS)]
+        sums = [bank(PACK + t) for t in range(PACK)]
+        for t in range(PACK):
+            open_group1(sums[t], t, 1)
+            close_group1(sums[t], t, 1)
+
+        def gather_items(chunk):
+            first = chunk * ITEM_CHUNK
+            for g in range(GROUPS):
                 nc.vector.tensor_copy(
-                    iw[a][:, c * ITEM_CHUNK : (c + 1) * ITEM_CHUNK],
-                    iw_win[a][:].bitcast(U32).indirect(items[:, c * ITEM_CHUNK // 16 : (c + 1) * ITEM_CHUNK // 16]),
+                    item_words[g][:, first : first + ITEM_CHUNK],
+                    item_table[g][:].bitcast(U32).indirect(entries(items, first, ITEM_CHUNK)),
                 )
 
-        def score(i, hf):
+        def score(i, half, pieces=1):
             acc = bank(i)
-            for a in range(GROUPS):
+            for g in range(GROUPS):
                 nc.tensor.matmul_mx(
                     out=acc[:],
-                    lhsT=iw[a][:, i * P : (i + 1) * P].bitcast(FP8X4),
-                    lhsT_scale=is_m[8 + 4 * a : P, :].bitcast(U8)[:, i * P : (i + 1) * P],
-                    rhs=hc[a][hf][:].bitcast(FP8X4),
-                    rhs_scale=hs[a][hf][:],
-                    start=a == 0,
-                    stop=a == GROUPS - 1,
+                    lhsT=item_words[g][:, i * P : (i + 1) * P].bitcast(FP8X4),
+                    lhsT_scale=item_plane[ITEM_SHIFT + ROWS * g : P, :].bitcast(U8)[:, i * P : (i + 1) * P],
+                    rhs=h_codes[g, half][:].bitcast(FP8X4),
+                    rhs_scale=h_plane[g, half][:],
+                    start=g == 0,
+                    stop=g == GROUPS - 1,
                 )
-            prob = ring.tile([P, NB], F32, name="prob")
-            pieces = 2 if (i, hf) == (S2 // P - 1, HALVES - 1) else 1
+            prob = results.tile([P, BANK], F32, name="prob")
             for s in range(pieces):
-                cols = slice(s * NB // pieces, (s + 1) * NB // pieces)
-                nc.scalar.activation(prob[:, cols], acc[:, cols], ACT.Sigmoid, bias=b2_cols[:, i : i + 1])
-                nc.sync.dma_start(out[i * P : (i + 1) * P, hf * NB : (hf + 1) * NB][:, cols], prob[:, cols])
+                columns = slice(s * BANK // pieces, (s + 1) * BANK // pieces)
+                nc.scalar.activation(prob[:, columns], acc[:, columns], ACT.Sigmoid, bias=b2_cols[:, i : i + 1])
+                nc.sync.dma_start(out[i * P : (i + 1) * P, half * BANK : (half + 1) * BANK][:, columns], prob[:, columns])
 
-        layer_group1(0)
-        quantize_h(0, 0)
-        iw += [sb("iw%d" % a, [P, S2], U32, ("slot_h", "slot_i")[a]) for a in range(GROUPS)]
-        layer_group1(1)
         gather_items(0)
         gather_items(1)
         quantize_h(1, 0)
-        for i in range(S2 // P):
-            if i == 4:
-                gather_items(2)
-                quantize_h(0, 1)
-            if i == 6:
-                quantize_h(1, 1)
-                gather_items(3)
+        for i in (0, 1, 2, 3):
             score(i, 0)
-        for i in range(S2 // P):
+        gather_items(2)
+        quantize_h(0, 1)
+        for i in (4, 5):
+            score(i, 0)
+        quantize_h(1, 1)
+        gather_items(3)
+        for i in (6, 7):
+            score(i, 0)
+        for i in range(ITEM_TILES - 1):
             score(i, 1)
+        score(ITEM_TILES - 1, 1, pieces=2)

@@ -35,6 +35,8 @@ ITEM_TILES = S2 // P
 ITEM_CHUNK = 2 * P
 ITEM_SHIFT = 8
 MOVES_AHEAD = 6
+SPLIT_TILES = 8
+LATE = 2 * T * BYTES + 2048
 PIECES = 2
 
 
@@ -45,7 +47,8 @@ def tile_list_listed_click_probabilities_kernel(
     with ExitStack() as ctx:
         lists = ctx.enter_context(tc.tile_pool(name="lists", bufs=1))
         keep = ctx.enter_context(tc.tile_pool(name="keep", bufs=1))
-        results = ctx.enter_context(tc.tile_pool(name="results", bufs=ITEM_TILES * HALVES))
+        results = ctx.enter_context(tc.tile_pool(name="results", bufs=ITEM_TILES * HALVES + SPLIT_TILES))
+        placed = ctx.enter_context(tc.tile_pool(name="placed", bufs=1))
         psum = ctx.enter_context(tc.psum_pool(name="psum", bufs=1))
 
         def sbuf(name, shape, dtype, tag=None):
@@ -60,38 +63,53 @@ def tile_list_listed_click_probabilities_kernel(
         users = lists.tile([P, S // PER_COLUMN], U16, name="users")
         items = lists.tile([P, S2 // PER_COLUMN], U16, name="items")
 
-        user_rows = sbuf("user_rows", [P, T // BYTES], I32, "shared_e")
+        user_rows = placed.tile([P, T // BYTES], I32, name="user_rows", align_bytes=64, offset=T * BYTES - T // 4)
         user_plane = [sbuf("user_plane%d" % a, [P, S // BYTES], I32) for a in range(USER_PASSES)]
         w4_plane_raw = sbuf("w4_plane_raw", [P, W4_PASSES, H // BYTES], I32, "shared_d")
         item_rows = sbuf("item_rows", [P, T2 // BYTES], I32, "shared_f")
-        b2_rows = sbuf("b2_rows", [P, P], F32, "shared_a")
+        b2_rows = sbuf("b2_rows", [P, P], F32)
         middle = T // BYTES // 2
-        nc.gpsimd.memset(b2_rows[:], 0.0)
         nc.gpsimd.memset(user_rows[:, :middle], 0)
+        nc.gpsimd.memset(b2_rows[:], 0.0)
         nc.vector.memset(user_rows[:, middle:], 0)
         nc.vector.memset(w4_plane_raw[:], 0)
         nc.vector.memset(item_rows[:], 0)
         for a in range(USER_PASSES):
             nc.vector.memset(user_plane[a][:], 0)
 
-        w4_raw = sbuf("w4_raw", [P, W4_PASSES, 2 * H // BYTES], I32)
-        nc.sync.dma_start(w4_raw[:], w4_words.rearrange("a p c -> p a c").bitcast(I32))
+        w4_view = w4_words.rearrange("a p c -> p a c").bitcast(I32)
+        w4_span = 2 * K_PASS // BYTES
+        w4_raw = [sbuf("w4_raw0", [P, W4_PASSES, w4_span], I32)]
+        nc.sync.dma_start(w4_raw[0][:], w4_view[:, :, 0:w4_span])
         nc.sync.dma_start(users[:], offs)
         nc.sync.dma_start(items[:], offs2)
         b1_cols = sbuf("b1_cols", [P, GROUPS, PACK], F32)
         nc.sync.dma_start(b1_cols[:], b1.rearrange("(g p t) -> p g t", p=P, t=PACK))
-        nc.sync.dma_start(b2_rows[0:ITEM_TILES, :], b2.rearrange("(i p) -> i p", p=P))
         nc.sync.dma_start(user_rows[0:P:4, :], tab_scales[1:3].rearrange("a q t -> (a q) t").bitcast(I32))
         nc.sync.dma_start(user_rows[2:P:8, :], tab_scales[0].bitcast(I32))
         w1_rows = w1.rearrange("(p j) c -> p j c", j=PACK)
-        w1_raw = [sbuf("w1_raw0", [P, PACK, K_PASS], F32, "shared_c")]
-        nc.sync.dma_start(w1_raw[0][:], w1_rows[:, :, 0:K_PASS])
+        nc.sync.dma_start(b2_rows[0:ITEM_TILES, :], b2.rearrange("(i p) -> i p", p=P))
+        user_table = [
+            sbuf("user_table0", [P, T], I32, "shared_a"),
+            sbuf("user_table1", [P, T], I32, "shared_e"),
+            placed.tile([P, T], I32, name="user_table2", align_bytes=64, offset=0),
+        ]
+
+        def load_user_pass(a, columns=slice(0, T)):
+            nc.sync.dma_start(user_table[a][:, columns], tab_words[a].rearrange("p t i -> p (t i)").bitcast(I32)[:, columns])
+
+        load_user_pass(0, slice(0, T // 2))
         for r in range(ROWS):
             nc.sync.dma_start(
                 w4_plane_raw[r:P:QUAD, :, :],
                 w4_scales[:, r : P // 8 : ROWS, :].rearrange("a q c -> q a c").bitcast(I32),
             )
-        nc.sync.dma_start(item_rows[0:P:4, :], tab2_scales.rearrange("a q t -> (a q) t").bitcast(I32))
+        load_user_pass(0, slice(T // 2, T))
+        for q in range(P // QUAD):
+            nc.sync.dma_start(
+                item_rows[QUAD * q + ITEM_SHIFT : QUAD * q + ITEM_SHIFT + GROUPS * ROWS, :],
+                tab2_scales[:, ROWS * q : ROWS * (q + 1), :].bitcast(I32),
+            )
 
         identity = sbuf("identity", [P, P], F32)
         make_identity(nc, identity[:])
@@ -100,23 +118,18 @@ def tile_list_listed_click_probabilities_kernel(
         b2_cols = sbuf("b2_cols", [P, ITEM_TILES], F32)
         nc.scalar.copy(b2_cols[:], b2_turned[:, 0:ITEM_TILES])
 
-        user_table = []
-
-        def load_user_pass(a, tag):
-            user_table.append(sbuf("user_table%d" % a, [P, T], I32, tag))
-            nc.sync.dma_start(user_table[a][:], tab_words[a].rearrange("p t i -> p (t i)").bitcast(I32))
-
-        load_user_pass(0, "shared_a")
+        load_user_pass(1)
 
         user_picked = sbuf("user_picked", [P, S // BYTES], I32)
         nc.vector.tensor_copy(user_picked[:].bitcast(U8), user_rows[:].bitcast(U8).indirect(users[:]))
-        moves = [(user_plane[0][r:P:QUAD, :], user_picked[2 + 8 * r : P : 32, :]) for r in range(ROWS)]
+        moves = []
         for a in range(1, USER_PASSES):
             moves += [(user_plane[a][r:P:QUAD, :], user_picked[64 * (a - 1) + 4 * r : 64 * a : 16, :]) for r in range(ROWS)]
+        moves += [(user_plane[0][r:P:QUAD, :], user_picked[2 + 8 * r : P : 32, :]) for r in range(ROWS)]
         for destination, source in moves[:MOVES_AHEAD]:
             nc.sync.dma_start(destination, source)
-        load_user_pass(1, "shared_e")
-        for destination, source in moves[MOVES_AHEAD:]:
+        load_user_pass(2)
+        for destination, source in moves[MOVES_AHEAD : 2 * ROWS]:
             nc.sync.dma_start(destination, source)
 
         def reorder_columns(ordered, raw):
@@ -125,29 +138,45 @@ def tile_list_listed_click_probabilities_kernel(
                 raw.rearrange("p (b m t) -> p b t m", t=PACK, m=P),
             )
 
-        w4_codes = sbuf("w4_codes", [P, W4_PASSES * 2 * H], U8)
+        w4_codes = [sbuf("w4_codes%d" % g, [P, W4_PASSES * 2 * K_PASS], U8) for g in range(GROUPS)]
         w4_plane = sbuf("w4_plane", [P, W4_PASSES * H], U8)
-        reorder_columns(w4_codes[:].bitcast(U16), w4_raw[:].rearrange("p a c -> p (a c)").bitcast(U16))
 
-        w1_codes = [sbuf("w1_codes%d" % g, [P, K_PASS], U32) for g in range(GROUPS)]
-        w1_plane = [sbuf("w1_plane%d" % g, [P, K_PASS], U8) for g in range(GROUPS)]
-        w1_bf16 = [sbuf("w1_bf16_0", [P, K_PASS * PACK], BF16, "shared_g"), sbuf("w1_bf16_1", [P, K_PASS * PACK], BF16)]
+        def reorder_w4(g):
+            reorder_columns(w4_codes[g][:].bitcast(U16), w4_raw[g][:].rearrange("p a c -> p (a c)").bitcast(U16))
 
-        def round_w1(g, copy):
+        reorder_w4(0)
+
+        w4_raw.append(placed.tile([P, W4_PASSES, w4_span], I32, name="w4_raw1", align_bytes=64, offset=T * BYTES))
+        w1_raw = placed.tile([P, PACK * H], F32, name="w1_raw", align_bytes=64, offset=T * BYTES + 2048)
+        w1_runs = [(0, K_PASS // 2), (K_PASS // 2, K_PASS // 2), (K_PASS, K_PASS)]
+
+        def w1_run(run):
+            first, count = w1_runs[run]
+            return w1_raw[:, PACK * first : PACK * (first + count)].rearrange("p (j c) -> p j c", j=PACK)
+
+        for run, (first, count) in enumerate(w1_runs):
+            if run == 2:
+                for destination, source in moves[2 * ROWS :]:
+                    nc.sync.dma_start(destination, source)
+                nc.sync.dma_start(w4_raw[1][:], w4_view[:, :, w4_span : 2 * w4_span])
+            nc.sync.dma_start(w1_run(run), w1_rows[:, :, first : first + count])
+        pairs = [(g, u) for g in range(GROUPS) for u in range(2)]
+        w1_bf16 = {k: sbuf("w1_bf16_%d_%d" % k, [P, 2 * K_PASS], BF16) for k in pairs}
+        w1_codes = {k: sbuf("w1_codes%d_%d" % k, [P, 2 * P], U32) for k in pairs}
+        w1_plane = {k: sbuf("w1_plane%d_%d" % k, [P, 2 * P], U8) for k in pairs}
+
+        def round_w1(run, u, copy):
+            first, count = w1_runs[run]
+            g, at = divmod(first, K_PASS)
             copy(
-                w1_bf16[g][:].rearrange("p (t m j) -> p m t j", t=PACK, j=PACK),
-                w1_raw[g][:].rearrange("p j (m t) -> p m t j", t=PACK),
+                w1_bf16[g, u][:].rearrange("p (t m j) -> p m t j", t=2, j=PACK)[:, at // PACK : (at + count) // PACK],
+                w1_run(run).rearrange("p j (m t) -> p m t j", t=PACK)[:, :, 2 * u : 2 * u + 2],
             )
 
-        def quantize_w1(g):
-            nc.vector.quantize_mx(out=w1_codes[g][:].bitcast(FP8X4), scales=w1_plane[g][:], in_=w1_bf16[g][:])
+        def quantize_w1(g, u):
+            nc.vector.quantize_mx(out=w1_codes[g, u][:].bitcast(FP8X4), scales=w1_plane[g, u][:], in_=w1_bf16[g, u][:])
 
-        round_w1(0, nc.scalar.copy)
-        load_user_pass(2, "shared_c")
-        item_picked = sbuf("item_picked", [P, S2 // BYTES], I32)
-        quantize_w1(0)
-        w1_raw.append(sbuf("w1_raw1", [P, PACK, K_PASS], F32, "shared_g"))
-        nc.sync.dma_start(w1_raw[1][:], w1_rows[:, :, K_PASS : 2 * K_PASS])
+        item_plane = sbuf("item_plane", [P, S2 // BYTES], I32)
 
         user_words = {}
         user_words_tag = {(1, 0): "shared_d", (2, 0): "shared_f"}
@@ -159,11 +188,12 @@ def tile_list_listed_click_probabilities_kernel(
 
         def layer_pass(acc, g, t, half, a, start, stop):
             if a == 0:
-                columns = slice(t * P, (t + 1) * P)
-                weights, weight_scales = w1_codes[g][:, columns].bitcast(FP8X4), w1_plane[g][:, columns]
+                columns = slice(t % 2 * P, (t % 2 + 1) * P)
+                weights, weight_scales = w1_codes[g, t // 2][:, columns].bitcast(FP8X4), w1_plane[g, t // 2][:, columns]
             else:
                 first = (a - 1) * H + (g * PACK + t) * P
-                weights = w4_codes[:, 2 * first : 2 * (first + P)].bitcast(FP4X4)
+                at = (a - 1) * K_PASS + t * P
+                weights = w4_codes[g][:, 2 * at : 2 * (at + P)].bitcast(FP4X4)
                 weight_scales = w4_plane[:, first : first + P]
             nc.tensor.matmul_mx(
                 out=acc[:],
@@ -176,61 +206,74 @@ def tile_list_listed_click_probabilities_kernel(
             )
 
         blocks = [(g, half) for g in range(GROUPS) for half in range(HALVES)]
-        h_tiles = {b: sbuf("h_tiles%d_%d" % b, [P, PACK, BANK], BF16, "shared_h" if b == (0, 0) else None) for b in blocks}
-        h_packed = {b: sbuf("h_packed%d_%d" % b, [P, BANK * PACK], BF16, "shared_i" if b == (0, 0) else None) for b in blocks}
+        h_tiles = {b: sbuf("h_tiles%d_%d" % b, [P, PACK, BANK], BF16, "shared_h" if b == (0, 0) else None) for b in blocks if b != (1, 0)}
+        h_tiles[1, 0] = placed.tile([P, PACK, BANK], BF16, name="h_tiles1_0", align_bytes=64, offset=LATE)
+        h_packed = {
+            (0, 0): placed.tile([P, BANK * PACK], BF16, name="h_packed0_0", align_bytes=64, offset=T * BYTES + 2048),
+            (1, 0): sbuf("h_packed1_0", [P, BANK * PACK], BF16),
+        }
         h_codes = {b: sbuf("h_codes%d_%d" % b, [P, BANK], U32) for b in blocks}
         h_plane = {b: sbuf("h_plane%d_%d" % b, [P, BANK], U8) for b in blocks}
 
         def relu_out(acc, g, t, half):
             nc.scalar.activation(h_tiles[g, half][:, t, :], acc[:], ACT.Relu, bias=b1_cols[:, g, t : t + 1])
 
+        width = BANK // PIECES
+
+        def interleave_h(g, half, s):
+            nc.vector.tensor_copy(
+                h_packed[g, half][:, s * width * PACK : (s + 1) * width * PACK].rearrange("p (c i t) -> p c t i", i=4, t=PACK),
+                h_tiles[g, half][:, :, s * width : (s + 1) * width].rearrange("p t (c i) -> p c t i", i=4),
+            )
+
+        def quantize_piece(g, half, s):
+            nc.vector.quantize_mx(
+                out=h_codes[g, half][:, s * width : (s + 1) * width].bitcast(FP8X4),
+                scales=h_plane[g, half][:, s * width : (s + 1) * width],
+                in_=h_packed[g, half][:, s * width * PACK : (s + 1) * width * PACK],
+            )
+
         def quantize_h(g, half):
-            width = BANK // PIECES
             for s in range(PIECES):
-                nc.vector.tensor_copy(
-                    h_packed[g, half][:, s * width * PACK : (s + 1) * width * PACK].rearrange(
-                        "p (c i t) -> p c t i", i=4, t=PACK
-                    ),
-                    h_tiles[g, half][:, :, s * width : (s + 1) * width].rearrange("p t (c i) -> p c t i", i=4),
-                )
+                interleave_h(g, half, s)
             for s in range(PIECES):
-                nc.vector.quantize_mx(
-                    out=h_codes[g, half][:, s * width : (s + 1) * width].bitcast(FP8X4),
-                    scales=h_plane[g, half][:, s * width : (s + 1) * width],
-                    in_=h_packed[g, half][:, s * width * PACK : (s + 1) * width * PACK],
-                )
+                quantize_piece(g, half, s)
 
         item_table = []
         group0 = [[bank(PACK * half + t) for t in range(PACK)] for half in range(HALVES)]
-        last_pass = USER_PASSES - 1
         for a in range(USER_PASSES):
             for half in range(HALVES):
                 gather_users(a, half)
-                for t in range(PACK):
-                    layer_pass(group0[half][t], 0, t, half, a, a == 0, a == last_pass)
-                    if a == last_pass:
-                        relu_out(group0[half][t], 0, t, half)
+                if a > 0:
+                    for t in range(PACK):
+                        layer_pass(group0[half][t], 0, t, half, a, a == 1, False)
             if a == 0:
                 reorder_columns(w4_plane[:], w4_plane_raw[:].rearrange("p a c -> p (a c)").bitcast(U8))
                 for first in (0, S2 // 2):
                     nc.vector.tensor_copy(
-                        item_picked[:].bitcast(U8)[:, first : first + S2 // 2],
+                        item_plane[:].bitcast(U8)[:, first : first + S2 // 2],
                         item_rows[:].bitcast(U8).indirect(entries(items, first, S2 // 2)),
                     )
-            if a < GROUPS:
-                item_table.append(sbuf("item_table%d" % a, [P, T2], I32, ("shared_a", "shared_e")[a]))
-                nc.sync.dma_start(item_table[a][:], tab2_words[a].rearrange("p t i -> p (t i)").bitcast(I32))
+        for a in range(GROUPS):
+            item_table.append(placed.tile([P, T2], I32, name="item_table%d" % a, align_bytes=64, offset=a * T2 * BYTES))
+            nc.sync.dma_start(item_table[a][:], tab2_words[a].rearrange("p t i -> p (t i)").bitcast(I32))
+        round_w1(0, 0, nc.scalar.copy)
+        round_w1(0, 1, nc.scalar.copy)
+        round_w1(1, 0, nc.scalar.copy)
+        round_w1(1, 1, nc.vector.tensor_copy)
+        quantize_w1(0, 0)
+        quantize_w1(0, 1)
+        reorder_w4(1)
+        for half in range(HALVES):
+            for t in range(PACK):
+                layer_pass(group0[half][t], 0, t, half, 0, False, True)
+        for t in range(PACK):
+            relu_out(group0[0][t], 0, t, 0)
 
-        round_w1(1, nc.vector.tensor_copy)
-        item_plane = sbuf("item_plane", [P, S2 // BYTES], I32, "shared_c")
-        nc.vector.memset(item_plane[:], 0)
-        for g in range(GROUPS):
-            for r in range(ROWS):
-                nc.sync.dma_start(
-                    item_plane[ITEM_SHIFT + ROWS * g + r : P : QUAD, :],
-                    item_picked[64 * g + 4 * r : 64 * (g + 1) : 16, :],
-                )
-        quantize_w1(1)
+        for u in range(2):
+            round_w1(2, u, nc.vector.tensor_copy)
+        for u in range(2):
+            quantize_w1(1, u)
 
         def open_group1(acc, t, half):
             for a in range(1, USER_PASSES):
@@ -243,54 +286,72 @@ def tile_list_listed_click_probabilities_kernel(
         sums = [bank(t) for t in range(PACK)]
         for t in range(PACK):
             open_group1(sums[t], t, 0)
-        for t in range(PACK):
             close_group1(sums[t], t, 0)
+        for t in range(PACK):
+            relu_out(group0[1][t], 0, t, 1)
         quantize_h(0, 0)
-        item_words = [sbuf("item_words%d" % g, [P, S2], U32, ("shared_h", "shared_i")[g]) for g in range(GROUPS)]
+        item_words = {
+            (0, 0): sbuf("item_words0_0", [P, S2 // 2], U32, "shared_h"),
+            (1, 0): placed.tile([P, S2 // 2], U32, name="item_words1_0", align_bytes=64, offset=T * BYTES + 2048),
+        }
         sums = [bank(PACK + t) for t in range(PACK)]
         for t in range(PACK):
             open_group1(sums[t], t, 1)
             close_group1(sums[t], t, 1)
 
-        def gather_items(chunk):
-            first = chunk * ITEM_CHUNK
-            for g in range(GROUPS):
-                nc.vector.tensor_copy(
-                    item_words[g][:, first : first + ITEM_CHUNK],
-                    item_table[g][:].bitcast(U32).indirect(entries(items, first, ITEM_CHUNK)),
-                )
+        item_chunks = [(0, S2 // 2), (S2 // 2, ITEM_CHUNK), (S2 // 2 + ITEM_CHUNK, ITEM_CHUNK)]
 
-        def score(i, half, pieces=1):
-            acc = bank(i)
+        def gather_items(g, chunk):
+            nc.vector.tensor_copy(
+                item_words[g, chunk][:],
+                item_table[g][:].bitcast(U32).indirect(entries(items, *item_chunks[chunk])),
+            )
+
+        def score(acc, i, half, columns, pieces=1):
+            part = max(c for c, (first, count) in enumerate(item_chunks) if first <= i * P)
+            at = i * P - item_chunks[part][0]
             for g in range(GROUPS):
                 nc.tensor.matmul_mx(
-                    out=acc[:],
-                    lhsT=item_words[g][:, i * P : (i + 1) * P].bitcast(FP8X4),
+                    out=acc[:, columns],
+                    lhsT=item_words[g, part][:, at : at + P].bitcast(FP8X4),
                     lhsT_scale=item_plane[ITEM_SHIFT + ROWS * g : P, :].bitcast(U8)[:, i * P : (i + 1) * P],
-                    rhs=h_codes[g, half][:].bitcast(FP8X4),
-                    rhs_scale=h_plane[g, half][:],
+                    rhs=h_codes[g, half][:, columns].bitcast(FP8X4),
+                    rhs_scale=h_plane[g, half][:, columns],
                     start=g == 0,
                     stop=g == GROUPS - 1,
                 )
-            prob = results.tile([P, BANK], F32, name="prob")
+            count = (columns.stop - columns.start) // pieces
             for s in range(pieces):
-                columns = slice(s * BANK // pieces, (s + 1) * BANK // pieces)
-                nc.scalar.activation(prob[:, columns], acc[:, columns], ACT.Sigmoid, bias=b2_cols[:, i : i + 1])
-                nc.sync.dma_start(out[i * P : (i + 1) * P, half * BANK : (half + 1) * BANK][:, columns], prob[:, columns])
+                first = columns.start + s * count
+                prob = results.tile([P, count], F32, name="prob")
+                nc.scalar.activation(prob[:], acc[:, first : first + count], ACT.Sigmoid, bias=b2_cols[:, i : i + 1])
+                nc.sync.dma_start(out[i * P : (i + 1) * P, half * BANK + first : half * BANK + first + count], prob[:])
 
-        gather_items(0)
-        gather_items(1)
+        whole = slice(0, BANK)
+        for g in range(GROUPS):
+            gather_items(g, 0)
         quantize_h(1, 0)
-        for i in (0, 1, 2, 3):
-            score(i, 0)
-        gather_items(2)
-        quantize_h(0, 1)
-        for i in (4, 5):
-            score(i, 0)
-        quantize_h(1, 1)
-        gather_items(3)
-        for i in (6, 7):
-            score(i, 0)
-        for i in range(ITEM_TILES - 1):
-            score(i, 1)
-        score(ITEM_TILES - 1, 1, pieces=2)
+        for chunk, (first, count) in enumerate(item_chunks):
+            for g in range(GROUPS):
+                if chunk > 0:
+                    item_words[g, chunk] = placed.tile(
+                        [P, ITEM_CHUNK], U32, name="item_words%d_%d" % (g, chunk), align_bytes=64, offset=LATE + (GROUPS * (chunk - 1) + g) * ITEM_CHUNK * BYTES
+                    )
+                    gather_items(g, chunk)
+            for i in range(first // P, (first + count) // P):
+                score(bank(i), i, 0, whole)
+        h_packed[0, 1] = placed.tile([P, BANK * PACK], BF16, name="h_packed0_1", align_bytes=64, offset=0)
+        h_packed[1, 1] = sbuf("h_packed1_1", [P, BANK * PACK], BF16)
+        sums = [bank(i) for i in range(ITEM_TILES)]
+        for s in range(PIECES):
+            for g in range(GROUPS):
+                interleave_h(g, 1, s)
+            for g in range(GROUPS):
+                quantize_piece(g, 1, s)
+            if s == 0:
+                for i in range(SPLIT_TILES):
+                    score(sums[i], i, 1, slice(0, width))
+        for i in range(SPLIT_TILES, ITEM_TILES):
+            score(sums[i], i, 1, whole)
+        for i in range(SPLIT_TILES):
+            score(sums[i], i, 1, slice(width, BANK))

@@ -35,7 +35,7 @@ ITEM_TILES = S2 // P
 ITEM_CHUNK = 2 * P
 ITEM_SHIFT = 8
 MOVES_AHEAD = 6
-SPLIT_TILES = 8
+SPLIT_TILES = 5
 LATE = 2 * T * BYTES + 2048
 PIECES = 2
 
@@ -86,7 +86,7 @@ def tile_list_listed_click_probabilities_kernel(
         b1_cols = sbuf("b1_cols", [P, GROUPS, PACK], F32)
         nc.sync.dma_start(b1_cols[:], b1.rearrange("(g p t) -> p g t", p=P, t=PACK))
         nc.sync.dma_start(user_rows[0:P:4, :], tab_scales[1:3].rearrange("a q t -> (a q) t").bitcast(I32))
-        nc.sync.dma_start(user_rows[2:P:8, :], tab_scales[0].bitcast(I32))
+        nc.sync.dma_start(user_rows[6:P:8, :], tab_scales[0].bitcast(I32))
         w1_rows = w1.rearrange("(p j) c -> p j c", j=PACK)
         nc.sync.dma_start(b2_rows[0:ITEM_TILES, :], b2.rearrange("(i p) -> i p", p=P))
         user_table = [
@@ -125,24 +125,24 @@ def tile_list_listed_click_probabilities_kernel(
         moves = []
         for a in range(1, USER_PASSES):
             moves += [(user_plane[a][r:P:QUAD, :], user_picked[64 * (a - 1) + 4 * r : 64 * a : 16, :]) for r in range(ROWS)]
-        moves += [(user_plane[0][r:P:QUAD, :], user_picked[2 + 8 * r : P : 32, :]) for r in range(ROWS)]
+        moves += [(user_plane[0][ROWS + r : P : QUAD, :], user_picked[6 + 8 * r : P : 32, :]) for r in range(ROWS)]
         for destination, source in moves[:MOVES_AHEAD]:
             nc.sync.dma_start(destination, source)
         load_user_pass(2)
         for destination, source in moves[MOVES_AHEAD : 2 * ROWS]:
             nc.sync.dma_start(destination, source)
 
-        def reorder_columns(ordered, raw):
+        def reorder_columns(ordered, raw, line):
             nc.vector.tensor_copy(
-                ordered.rearrange("p (b t m) -> p b t m", t=PACK, m=P),
-                raw.rearrange("p (b m t) -> p b t m", t=PACK, m=P),
+                ordered.rearrange("p (b t c i) -> p b c t i", t=PACK, c=P // line, i=line),
+                raw.rearrange("p (b c i t) -> p b c t i", t=PACK, c=P // line, i=line),
             )
 
         w4_codes = [sbuf("w4_codes%d" % g, [P, W4_PASSES * 2 * K_PASS], U8) for g in range(GROUPS)]
         w4_plane = sbuf("w4_plane", [P, W4_PASSES * H], U8)
 
         def reorder_w4(g):
-            reorder_columns(w4_codes[g][:].bitcast(U16), w4_raw[g][:].rearrange("p a c -> p (a c)").bitcast(U16))
+            reorder_columns(w4_codes[g][:].bitcast(U16), w4_raw[g][:].rearrange("p a c -> p (a c)").bitcast(U16), 8)
 
         reorder_w4(0)
 
@@ -160,21 +160,26 @@ def tile_list_listed_click_probabilities_kernel(
                     nc.sync.dma_start(destination, source)
                 nc.sync.dma_start(w4_raw[1][:], w4_view[:, :, w4_span : 2 * w4_span])
             nc.sync.dma_start(w1_run(run), w1_rows[:, :, first : first + count])
-        pairs = [(g, u) for g in range(GROUPS) for u in range(2)]
-        w1_bf16 = {k: sbuf("w1_bf16_%d_%d" % k, [P, 2 * K_PASS], BF16) for k in pairs}
-        w1_codes = {k: sbuf("w1_codes%d_%d" % k, [P, 2 * P], U32) for k in pairs}
-        w1_plane = {k: sbuf("w1_plane%d_%d" % k, [P, 2 * P], U8) for k in pairs}
+        w1_bf16 = [sbuf("w1_bf16_%d" % g, [P, PACK * K_PASS], BF16) for g in range(GROUPS)]
+        w1_codes = [sbuf("w1_codes%d" % g, [P, K_PASS], U32) for g in range(GROUPS)]
+        w1_plane = [sbuf("w1_plane%d" % g, [P, K_PASS], U8) for g in range(GROUPS)]
 
-        def round_w1(run, u, copy):
+        def round_w1(run, copy, part=0, parts=1):
             first, count = w1_runs[run]
             g, at = divmod(first, K_PASS)
+            share = count // PACK // parts
             copy(
-                w1_bf16[g, u][:].rearrange("p (t m j) -> p m t j", t=2, j=PACK)[:, at // PACK : (at + count) // PACK],
-                w1_run(run).rearrange("p j (m t) -> p m t j", t=PACK)[:, :, 2 * u : 2 * u + 2],
+                w1_bf16[g][:].rearrange("p (t m j) -> p m t j", t=PACK, j=PACK)[:, at // PACK + part * share : at // PACK + (part + 1) * share],
+                w1_run(run).rearrange("p j (m t) -> p m t j", t=PACK)[:, part * share : (part + 1) * share],
             )
 
-        def quantize_w1(g, u):
-            nc.vector.quantize_mx(out=w1_codes[g, u][:].bitcast(FP8X4), scales=w1_plane[g, u][:], in_=w1_bf16[g, u][:])
+        def quantize_w1(g, tiles):
+            columns = slice(tiles.start * P, tiles.stop * P)
+            nc.vector.quantize_mx(
+                out=w1_codes[g][:, columns].bitcast(FP8X4),
+                scales=w1_plane[g][:, columns],
+                in_=w1_bf16[g][:, PACK * columns.start : PACK * columns.stop],
+            )
 
         item_plane = sbuf("item_plane", [P, S2 // BYTES], I32)
 
@@ -188,8 +193,8 @@ def tile_list_listed_click_probabilities_kernel(
 
         def layer_pass(acc, g, t, half, a, start, stop):
             if a == 0:
-                columns = slice(t % 2 * P, (t % 2 + 1) * P)
-                weights, weight_scales = w1_codes[g, t // 2][:, columns].bitcast(FP8X4), w1_plane[g, t // 2][:, columns]
+                columns = slice(t * P, (t + 1) * P)
+                weights, weight_scales = w1_codes[g][:, columns].bitcast(FP8X4), w1_plane[g][:, columns]
             else:
                 first = (a - 1) * H + (g * PACK + t) * P
                 at = (a - 1) * K_PASS + t * P
@@ -200,7 +205,7 @@ def tile_list_listed_click_probabilities_kernel(
                 lhsT=weights,
                 lhsT_scale=weight_scales,
                 rhs=user_words[a, half][:].bitcast(FP8X4),
-                rhs_scale=user_plane[a][:].bitcast(U8)[:, half * BANK : (half + 1) * BANK],
+                rhs_scale=user_plane[a][ROWS if a == 0 else 0 : P, :].bitcast(U8)[:, half * BANK : (half + 1) * BANK],
                 start=start,
                 stop=stop,
             )
@@ -248,7 +253,7 @@ def tile_list_listed_click_probabilities_kernel(
                     for t in range(PACK):
                         layer_pass(group0[half][t], 0, t, half, a, a == 1, False)
             if a == 0:
-                reorder_columns(w4_plane[:], w4_plane_raw[:].rearrange("p a c -> p (a c)").bitcast(U8))
+                reorder_columns(w4_plane[:], w4_plane_raw[:].rearrange("p a c -> p (a c)").bitcast(U8), 16)
                 for first in (0, S2 // 2):
                     nc.vector.tensor_copy(
                         item_plane[:].bitcast(U8)[:, first : first + S2 // 2],
@@ -257,12 +262,12 @@ def tile_list_listed_click_probabilities_kernel(
         for a in range(GROUPS):
             item_table.append(placed.tile([P, T2], I32, name="item_table%d" % a, align_bytes=64, offset=a * T2 * BYTES))
             nc.sync.dma_start(item_table[a][:], tab2_words[a].rearrange("p t i -> p (t i)").bitcast(I32))
-        round_w1(0, 0, nc.scalar.copy)
-        round_w1(0, 1, nc.scalar.copy)
-        round_w1(1, 0, nc.scalar.copy)
-        round_w1(1, 1, nc.vector.tensor_copy)
-        quantize_w1(0, 0)
-        quantize_w1(0, 1)
+        round_w1(0, nc.scalar.copy)
+        round_w1(1, nc.scalar.copy, 0, 2)
+        round_w1(1, nc.vector.tensor_copy, 1, 2)
+        quantize_w1(0, slice(0, 1))
+        quantize_w1(0, slice(1, 2))
+        quantize_w1(0, slice(2, 4))
         reorder_w4(1)
         for half in range(HALVES):
             for t in range(PACK):
@@ -270,10 +275,9 @@ def tile_list_listed_click_probabilities_kernel(
         for t in range(PACK):
             relu_out(group0[0][t], 0, t, 0)
 
+        round_w1(2, nc.vector.tensor_copy)
         for u in range(2):
-            round_w1(2, u, nc.vector.tensor_copy)
-        for u in range(2):
-            quantize_w1(1, u)
+            quantize_w1(1, slice(2 * u, 2 * u + 2))
 
         def open_group1(acc, t, half):
             for a in range(1, USER_PASSES):

@@ -37,6 +37,7 @@ ITEM_SHIFT = 8
 MOVES_AHEAD = 6
 SPLIT_TILES = 5
 LATE = 2 * T * BYTES + 2048
+SCALAR_SHARE = 56
 PIECES = 2
 
 
@@ -47,7 +48,7 @@ def tile_list_listed_click_probabilities_kernel(
     with ExitStack() as ctx:
         lists = ctx.enter_context(tc.tile_pool(name="lists", bufs=1))
         keep = ctx.enter_context(tc.tile_pool(name="keep", bufs=1))
-        results = ctx.enter_context(tc.tile_pool(name="results", bufs=ITEM_TILES * HALVES + SPLIT_TILES))
+        results = ctx.enter_context(tc.tile_pool(name="results", bufs=13))
         placed = ctx.enter_context(tc.tile_pool(name="placed", bufs=1))
         psum = ctx.enter_context(tc.psum_pool(name="psum", bufs=1))
 
@@ -129,7 +130,7 @@ def tile_list_listed_click_probabilities_kernel(
         for destination, source in moves[:MOVES_AHEAD]:
             nc.sync.dma_start(destination, source)
         load_user_pass(2)
-        for destination, source in moves[MOVES_AHEAD : 2 * ROWS]:
+        for destination, source in moves[MOVES_AHEAD:]:
             nc.sync.dma_start(destination, source)
 
         def reorder_columns(ordered, raw, line):
@@ -148,29 +149,24 @@ def tile_list_listed_click_probabilities_kernel(
 
         w4_raw.append(placed.tile([P, W4_PASSES, w4_span], I32, name="w4_raw1", align_bytes=64, offset=T * BYTES))
         w1_raw = placed.tile([P, PACK * H], F32, name="w1_raw", align_bytes=64, offset=T * BYTES + 2048)
-        w1_runs = [(0, K_PASS // 2), (K_PASS // 2, K_PASS // 2), (K_PASS, K_PASS)]
+        w1_runs = [(0, K_PASS), (K_PASS, K_PASS)]
 
         def w1_run(run):
             first, count = w1_runs[run]
             return w1_raw[:, PACK * first : PACK * (first + count)].rearrange("p (j c) -> p j c", j=PACK)
 
         for run, (first, count) in enumerate(w1_runs):
-            if run == 2:
-                for destination, source in moves[2 * ROWS :]:
-                    nc.sync.dma_start(destination, source)
+            if run == 1:
                 nc.sync.dma_start(w4_raw[1][:], w4_view[:, :, w4_span : 2 * w4_span])
             nc.sync.dma_start(w1_run(run), w1_rows[:, :, first : first + count])
         w1_bf16 = [sbuf("w1_bf16_%d" % g, [P, PACK * K_PASS], BF16) for g in range(GROUPS)]
         w1_codes = [sbuf("w1_codes%d" % g, [P, K_PASS], U32) for g in range(GROUPS)]
         w1_plane = [sbuf("w1_plane%d" % g, [P, K_PASS], U8) for g in range(GROUPS)]
 
-        def round_w1(run, copy, part=0, parts=1):
-            first, count = w1_runs[run]
-            g, at = divmod(first, K_PASS)
-            share = count // PACK // parts
+        def round_w1(g, copy, share):
             copy(
-                w1_bf16[g][:].rearrange("p (t m j) -> p m t j", t=PACK, j=PACK)[:, at // PACK + part * share : at // PACK + (part + 1) * share],
-                w1_run(run).rearrange("p j (m t) -> p m t j", t=PACK)[:, part * share : (part + 1) * share],
+                w1_bf16[g][:].rearrange("p (t m j) -> p m t j", t=PACK, j=PACK)[:, share],
+                w1_run(g).rearrange("p j (m t) -> p m t j", t=PACK)[:, share],
             )
 
         def quantize_w1(g, tiles):
@@ -262,9 +258,8 @@ def tile_list_listed_click_probabilities_kernel(
         for a in range(GROUPS):
             item_table.append(placed.tile([P, T2], I32, name="item_table%d" % a, align_bytes=64, offset=a * T2 * BYTES))
             nc.sync.dma_start(item_table[a][:], tab2_words[a].rearrange("p t i -> p (t i)").bitcast(I32))
-        round_w1(0, nc.scalar.copy)
-        round_w1(1, nc.scalar.copy, 0, 2)
-        round_w1(1, nc.vector.tensor_copy, 1, 2)
+        round_w1(0, nc.scalar.copy, slice(0, SCALAR_SHARE))
+        round_w1(0, nc.vector.tensor_copy, slice(SCALAR_SHARE, P))
         quantize_w1(0, slice(0, 1))
         quantize_w1(0, slice(1, 2))
         quantize_w1(0, slice(2, 4))
@@ -275,7 +270,7 @@ def tile_list_listed_click_probabilities_kernel(
         for t in range(PACK):
             relu_out(group0[0][t], 0, t, 0)
 
-        round_w1(2, nc.vector.tensor_copy)
+        round_w1(1, nc.vector.tensor_copy, slice(0, P))
         for u in range(2):
             quantize_w1(1, slice(2 * u, 2 * u + 2))
 
@@ -311,25 +306,28 @@ def tile_list_listed_click_probabilities_kernel(
                 item_table[g][:].bitcast(U32).indirect(entries(items, *item_chunks[chunk])),
             )
 
-        def score(acc, i, half, columns, pieces=1):
-            part = max(c for c, (first, count) in enumerate(item_chunks) if first <= i * P)
-            at = i * P - item_chunks[part][0]
-            for g in range(GROUPS):
-                nc.tensor.matmul_mx(
-                    out=acc[:, columns],
-                    lhsT=item_words[g, part][:, at : at + P].bitcast(FP8X4),
-                    lhsT_scale=item_plane[ITEM_SHIFT + ROWS * g : P, :].bitcast(U8)[:, i * P : (i + 1) * P],
-                    rhs=h_codes[g, half][:, columns].bitcast(FP8X4),
-                    rhs_scale=h_plane[g, half][:, columns],
-                    start=g == 0,
-                    stop=g == GROUPS - 1,
-                )
-            count = (columns.stop - columns.start) // pieces
-            for s in range(pieces):
-                first = columns.start + s * count
-                prob = results.tile([P, count], F32, name="prob")
-                nc.scalar.activation(prob[:], acc[:, first : first + count], ACT.Sigmoid, bias=b2_cols[:, i : i + 1])
-                nc.sync.dma_start(out[i * P : (i + 1) * P, half * BANK + first : half * BANK + first + count], prob[:])
+        def score(sums, tiles, half, columns):
+            count = columns.stop - columns.start
+            prob = results.tile([P, len(tiles), count], F32, name="prob")
+            for n, i in enumerate(tiles):
+                part = max(c for c, (first, size) in enumerate(item_chunks) if first <= i * P)
+                at = i * P - item_chunks[part][0]
+                for g in range(GROUPS):
+                    nc.tensor.matmul_mx(
+                        out=sums[i][:, columns],
+                        lhsT=item_words[g, part][:, at : at + P].bitcast(FP8X4),
+                        lhsT_scale=item_plane[ITEM_SHIFT + ROWS * g : P, :].bitcast(U8)[:, i * P : (i + 1) * P],
+                        rhs=h_codes[g, half][:, columns].bitcast(FP8X4),
+                        rhs_scale=h_plane[g, half][:, columns],
+                        start=g == 0,
+                        stop=g == GROUPS - 1,
+                    )
+                nc.scalar.activation(prob[:, n, :], sums[i][:, columns], ACT.Sigmoid, bias=b2_cols[:, i : i + 1])
+            rows = out[tiles[0] * P : (tiles[-1] + 1) * P, half * BANK + columns.start : half * BANK + columns.stop]
+            nc.sync.dma_start(rows.rearrange("(n p) c -> p n c", p=P), prob[:])
+
+        def in_pairs(tiles):
+            return [tiles[n : n + 2] for n in range(0, len(tiles), 2)]
 
         whole = slice(0, BANK)
         for g in range(GROUPS):
@@ -342,8 +340,10 @@ def tile_list_listed_click_probabilities_kernel(
                         [P, ITEM_CHUNK], U32, name="item_words%d_%d" % (g, chunk), align_bytes=64, offset=LATE + (GROUPS * (chunk - 1) + g) * ITEM_CHUNK * BYTES
                     )
                     gather_items(g, chunk)
-            for i in range(first // P, (first + count) // P):
-                score(bank(i), i, 0, whole)
+            tiles = list(range(first // P, (first + count) // P))
+            sums = {i: bank(i) for i in tiles}
+            for pair in ([[0], [1], [2, 3]] if chunk == 0 else in_pairs(tiles)):
+                score(sums, pair, 0, whole)
         h_packed[0, 1] = placed.tile([P, BANK * PACK], BF16, name="h_packed0_1", align_bytes=64, offset=0)
         h_packed[1, 1] = sbuf("h_packed1_1", [P, BANK * PACK], BF16)
         sums = [bank(i) for i in range(ITEM_TILES)]
@@ -353,9 +353,9 @@ def tile_list_listed_click_probabilities_kernel(
             for g in range(GROUPS):
                 quantize_piece(g, 1, s)
             if s == 0:
-                for i in range(SPLIT_TILES):
-                    score(sums[i], i, 1, slice(0, width))
-        for i in range(SPLIT_TILES, ITEM_TILES):
-            score(sums[i], i, 1, whole)
-        for i in range(SPLIT_TILES):
-            score(sums[i], i, 1, slice(width, BANK))
+                for pair in in_pairs(list(range(SPLIT_TILES))):
+                    score(sums, pair, 1, slice(0, width))
+        for pair in in_pairs(list(range(SPLIT_TILES, ITEM_TILES))):
+            score(sums, pair, 1, whole)
+        for pair in in_pairs(list(range(SPLIT_TILES))):
+            score(sums, pair, 1, slice(width, BANK))

@@ -17,6 +17,7 @@ U8 = mybir.dt.uint8
 FP8X4 = mybir.dt.float8_e4m3fn_x4
 FP4X4 = mybir.dt.float4_e2m1fn_x4
 ACT = mybir.ActivationFunctionType
+ALU = mybir.AluOpType
 
 P = 128
 PACK = 4
@@ -35,7 +36,7 @@ ITEM_TILES = S2 // P
 ITEM_CHUNK = 2 * P
 ITEM_SHIFT = 8
 MOVES_AHEAD = 6
-SPLIT_TILES = 5
+SPLIT_TILES = 6
 LATE = 2 * T * BYTES + 2048
 SCALAR_SHARE = 56
 PIECES = 2
@@ -149,7 +150,7 @@ def tile_list_listed_click_probabilities_kernel(
 
         w4_raw.append(placed.tile([P, W4_PASSES, w4_span], I32, name="w4_raw1", align_bytes=64, offset=T * BYTES))
         w1_raw = placed.tile([P, PACK * H], F32, name="w1_raw", align_bytes=64, offset=T * BYTES + 2048)
-        w1_runs = [(0, K_PASS), (K_PASS, K_PASS)]
+        w1_runs = [(0, K_PASS), (K_PASS, K_PASS // 2), (3 * K_PASS // 2, K_PASS // 2)]
 
         def w1_run(run):
             first, count = w1_runs[run]
@@ -163,10 +164,11 @@ def tile_list_listed_click_probabilities_kernel(
         w1_codes = [sbuf("w1_codes%d" % g, [P, K_PASS], U32) for g in range(GROUPS)]
         w1_plane = [sbuf("w1_plane%d" % g, [P, K_PASS], U8) for g in range(GROUPS)]
 
-        def round_w1(g, copy, share):
+        def round_w1(run, copy, share):
+            g, at = divmod(w1_runs[run][0], K_PASS)
             copy(
-                w1_bf16[g][:].rearrange("p (t m j) -> p m t j", t=PACK, j=PACK)[:, share],
-                w1_run(g).rearrange("p j (m t) -> p m t j", t=PACK)[:, share],
+                w1_bf16[g][:].rearrange("p (t m j) -> p m t j", t=PACK, j=PACK)[:, at // PACK + share.start : at // PACK + share.stop],
+                w1_run(run).rearrange("p j (m t) -> p m t j", t=PACK)[:, share],
             )
 
         def quantize_w1(g, tiles):
@@ -208,7 +210,7 @@ def tile_list_listed_click_probabilities_kernel(
 
         blocks = [(g, half) for g in range(GROUPS) for half in range(HALVES)]
         h_tiles = {b: sbuf("h_tiles%d_%d" % b, [P, PACK, BANK], BF16, "shared_h" if b == (0, 0) else None) for b in blocks if b != (1, 0)}
-        h_tiles[1, 0] = placed.tile([P, PACK, BANK], BF16, name="h_tiles1_0", align_bytes=64, offset=LATE)
+        h_tiles[1, 0] = placed.tile([P, 2, PACK, BANK], BF16, name="h_tiles1_0", align_bytes=64, offset=LATE)[:, 0]
         h_packed = {
             (0, 0): placed.tile([P, BANK * PACK], BF16, name="h_packed0_0", align_bytes=64, offset=T * BYTES + 2048),
             (1, 0): sbuf("h_packed1_0", [P, BANK * PACK], BF16),
@@ -217,7 +219,11 @@ def tile_list_listed_click_probabilities_kernel(
         h_plane = {b: sbuf("h_plane%d_%d" % b, [P, BANK], U8) for b in blocks}
 
         def relu_out(acc, g, t, half):
-            nc.scalar.activation(h_tiles[g, half][:, t, :], acc[:], ACT.Relu, bias=b1_cols[:, g, t : t + 1])
+            bias = b1_cols[:, g, t : t + 1]
+            if (g, half, t) == (0, 0, PACK - 1):
+                nc.vector.tensor_scalar(h_tiles[g, half][:, t, :], acc[:], bias, 0.0, ALU.add, ALU.max)
+            else:
+                nc.scalar.activation(h_tiles[g, half][:, t, :], acc[:], ACT.Relu, bias=bias)
 
         width = BANK // PIECES
 
@@ -270,9 +276,11 @@ def tile_list_listed_click_probabilities_kernel(
         for t in range(PACK):
             relu_out(group0[0][t], 0, t, 0)
 
-        round_w1(1, nc.vector.tensor_copy, slice(0, P))
-        for u in range(2):
-            quantize_w1(1, slice(2 * u, 2 * u + 2))
+        round_w1(1, nc.vector.tensor_copy, slice(0, P // 2))
+        round_w1(2, nc.vector.tensor_copy, slice(0, P // 2))
+        quantize_w1(1, slice(0, 1))
+        quantize_w1(1, slice(1, 2))
+        quantize_w1(1, slice(2, PACK))
 
         def open_group1(acc, t, half):
             for a in range(1, USER_PASSES):
@@ -283,28 +291,32 @@ def tile_list_listed_click_probabilities_kernel(
             relu_out(acc, 1, t, half)
 
         sums = [bank(t) for t in range(PACK)]
-        for t in range(PACK):
-            open_group1(sums[t], t, 0)
-            close_group1(sums[t], t, 0)
+        for t in range(PACK + 2):
+            if t < PACK:
+                open_group1(sums[t], t, 0)
+            if t >= 2:
+                close_group1(sums[t - 2], t - 2, 0)
         for t in range(PACK):
             relu_out(group0[1][t], 0, t, 1)
         quantize_h(0, 0)
-        item_words = {
-            (0, 0): sbuf("item_words0_0", [P, S2 // 2], U32, "shared_h"),
-            (1, 0): placed.tile([P, S2 // 2], U32, name="item_words1_0", align_bytes=64, offset=T * BYTES + 2048),
-        }
+        early_items = sbuf("early_items", [P, 2 * ITEM_CHUNK], U32, "shared_h")
+        item_words = {(0, chunk): early_items[:, chunk * ITEM_CHUNK : (chunk + 1) * ITEM_CHUNK] for chunk in range(2)}
         sums = [bank(PACK + t) for t in range(PACK)]
-        for t in range(PACK):
+        for t in range(PACK - 1):
             open_group1(sums[t], t, 1)
             close_group1(sums[t], t, 1)
 
-        item_chunks = [(0, S2 // 2), (S2 // 2, ITEM_CHUNK), (S2 // 2 + ITEM_CHUNK, ITEM_CHUNK)]
+        item_chunks = [(first, ITEM_CHUNK) for first in range(0, S2, ITEM_CHUNK)]
 
-        def gather_items(g, chunk):
-            nc.vector.tensor_copy(
-                item_words[g, chunk][:],
-                item_table[g][:].bitcast(U32).indirect(entries(items, *item_chunks[chunk])),
+        def gather_items(words, g, first, count):
+            nc.vector.tensor_copy(words, item_table[g][:].bitcast(U32).indirect(entries(items, first, count)))
+
+        def gather_late(g, chunk):
+            words = placed.tile(
+                [P, ITEM_CHUNK], U32, name="item_words%d_%d" % (g, chunk), align_bytes=64, offset=LATE + (len(item_words) - 3) * ITEM_CHUNK * BYTES
             )
+            item_words[g, chunk] = words[:]
+            gather_items(words[:], g, chunk * ITEM_CHUNK, ITEM_CHUNK)
 
         def score(sums, tiles, half, columns):
             count = columns.stop - columns.start
@@ -330,20 +342,23 @@ def tile_list_listed_click_probabilities_kernel(
             return [tiles[n : n + 2] for n in range(0, len(tiles), 2)]
 
         whole = slice(0, BANK)
-        for g in range(GROUPS):
-            gather_items(g, 0)
+        gather_items(early_items[:], 0, 0, 2 * ITEM_CHUNK)
+        first_items = placed.tile([P, ITEM_CHUNK], U32, name="first_items", align_bytes=64, offset=T * BYTES + 2048)
+        item_words[1, 0] = first_items[:]
+        gather_items(first_items[:], 1, 0, ITEM_CHUNK)
         quantize_h(1, 0)
         for chunk, (first, count) in enumerate(item_chunks):
             for g in range(GROUPS):
-                if chunk > 0:
-                    item_words[g, chunk] = placed.tile(
-                        [P, ITEM_CHUNK], U32, name="item_words%d_%d" % (g, chunk), align_bytes=64, offset=LATE + (GROUPS * (chunk - 1) + g) * ITEM_CHUNK * BYTES
-                    )
-                    gather_items(g, chunk)
+                if (g, chunk) not in item_words:
+                    gather_late(g, chunk)
             tiles = list(range(first // P, (first + count) // P))
             sums = {i: bank(i) for i in tiles}
-            for pair in ([[0], [1], [2, 3]] if chunk == 0 else in_pairs(tiles)):
+            for pair in ([[0], [1]] if chunk == 0 else in_pairs(tiles)):
                 score(sums, pair, 0, whole)
+            if chunk == 0:
+                last_sum = bank(0)
+                open_group1(last_sum, PACK - 1, 1)
+                close_group1(last_sum, PACK - 1, 1)
         h_packed[0, 1] = placed.tile([P, BANK * PACK], BF16, name="h_packed0_1", align_bytes=64, offset=0)
         h_packed[1, 1] = sbuf("h_packed1_1", [P, BANK * PACK], BF16)
         sums = [bank(i) for i in range(ITEM_TILES)]

@@ -79,6 +79,10 @@ def tile_list_listed_click_probabilities_kernel(
         for a in range(USER_PASSES):
             nc.vector.memset(user_plane[a][:], 0)
 
+        warm = sbuf("warm", [P, 2], F32)
+        nc.vector.memset(warm[:], 0.0)
+        nc.scalar.activation(warm[:, 1:2], warm[:, 0:1], ACT.Sigmoid)
+
         w4_view = w4_words.rearrange("a p c -> p a c").bitcast(I32)
         w4_span = 2 * K_PASS // BYTES
         w4_raw = [sbuf("w4_raw0", [P, W4_PASSES, w4_span], I32)]

@@ -54,7 +54,7 @@ def tile_list_listed_click_probabilities_kernel(
         psum = ctx.enter_context(tc.psum_pool(name="psum", bufs=1))
 
         def sbuf(name, shape, dtype, tag=None):
-            return keep.tile(shape, dtype, name=name, tag=tag or name, align_bytes=64)
+            return keep.tile(shape, dtype, name=name, tag=tag or name, align_bytes=256)
 
         def bank(b, columns=BANK):
             return psum.tile([P, columns], F32, name="bank%d" % b)
@@ -65,7 +65,7 @@ def tile_list_listed_click_probabilities_kernel(
         users = lists.tile([P, S // PER_COLUMN], U16, name="users")
         items = lists.tile([P, S2 // PER_COLUMN], U16, name="items")
 
-        user_rows = placed.tile([P, T // BYTES], I32, name="user_rows", align_bytes=64, offset=T * BYTES - T // 4)
+        user_rows = placed.tile([P, T // BYTES], I32, name="user_rows", align_bytes=256, offset=T * BYTES - T // 4)
         user_plane = [sbuf("user_plane%d" % a, [P, S // BYTES], I32) for a in range(USER_PASSES)]
         w4_plane_raw = sbuf("w4_plane_raw", [P, W4_PASSES, H // BYTES], I32, "shared_d")
         item_rows = sbuf("item_rows", [P, T2 // BYTES], I32, "shared_f")
@@ -78,10 +78,8 @@ def tile_list_listed_click_probabilities_kernel(
         nc.vector.memset(item_rows[:], 0)
         for a in range(USER_PASSES):
             nc.vector.memset(user_plane[a][:], 0)
-
-        warm = sbuf("warm", [P, 2], F32)
-        nc.vector.memset(warm[:], 0.0)
-        nc.scalar.activation(warm[:, 1:2], warm[:, 0:1], ACT.Sigmoid)
+        item_plane = sbuf("item_plane", [P, S2 // BYTES], I32)
+        nc.vector.memset(item_plane[:], 0)
 
         w4_view = w4_words.rearrange("a p c -> p a c").bitcast(I32)
         w4_span = 2 * K_PASS // BYTES
@@ -98,7 +96,7 @@ def tile_list_listed_click_probabilities_kernel(
         user_table = [
             sbuf("user_table0", [P, T], I32, "shared_a"),
             sbuf("user_table1", [P, T], I32, "shared_e"),
-            placed.tile([P, T], I32, name="user_table2", align_bytes=64, offset=0),
+            placed.tile([P, T], I32, name="user_table2", align_bytes=256, offset=0),
         ]
 
         def load_user_pass(a, columns=slice(0, T)):
@@ -111,11 +109,7 @@ def tile_list_listed_click_probabilities_kernel(
                 w4_scales[:, r : P // 8 : ROWS, :].rearrange("a q c -> q a c").bitcast(I32),
             )
         load_user_pass(0, slice(T // 2, T))
-        for q in range(P // QUAD):
-            nc.sync.dma_start(
-                item_rows[QUAD * q + ITEM_SHIFT : QUAD * q + ITEM_SHIFT + GROUPS * ROWS, :],
-                tab2_scales[:, ROWS * q : ROWS * (q + 1), :].bitcast(I32),
-            )
+        nc.sync.dma_start(item_rows[0:P:4, :], tab2_scales.rearrange("a q t -> (a q) t").bitcast(I32))
 
         identity = sbuf("identity", [P, P], F32)
         make_identity(nc, identity[:])
@@ -152,8 +146,8 @@ def tile_list_listed_click_probabilities_kernel(
 
         reorder_w4(0)
 
-        w4_raw.append(placed.tile([P, W4_PASSES, w4_span], I32, name="w4_raw1", align_bytes=64, offset=T * BYTES))
-        w1_raw = placed.tile([P, PACK * H], F32, name="w1_raw", align_bytes=64, offset=T * BYTES + 2048)
+        w4_raw.append(placed.tile([P, W4_PASSES, w4_span], I32, name="w4_raw1", align_bytes=256, offset=T * BYTES))
+        w1_raw = placed.tile([P, PACK * H], F32, name="w1_raw", align_bytes=256, offset=T * BYTES + 2048)
         w1_runs = [(0, K_PASS), (K_PASS, K_PASS // 2), (3 * K_PASS // 2, K_PASS // 2)]
 
         def w1_run(run):
@@ -183,7 +177,7 @@ def tile_list_listed_click_probabilities_kernel(
                 in_=w1_bf16[g][:, PACK * columns.start : PACK * columns.stop],
             )
 
-        item_plane = sbuf("item_plane", [P, S2 // BYTES], I32)
+        item_picked = sbuf("item_picked", [P, S2 // BYTES], I32)
 
         user_words = {}
         user_words_tag = {(1, 0): "shared_d", (2, 0): "shared_f"}
@@ -214,9 +208,9 @@ def tile_list_listed_click_probabilities_kernel(
 
         blocks = [(g, half) for g in range(GROUPS) for half in range(HALVES)]
         h_tiles = {b: sbuf("h_tiles%d_%d" % b, [P, PACK, BANK], BF16, "shared_h" if b == (0, 0) else None) for b in blocks if b != (1, 0)}
-        h_tiles[1, 0] = placed.tile([P, 2, PACK, BANK], BF16, name="h_tiles1_0", align_bytes=64, offset=LATE)[:, 0]
+        h_tiles[1, 0] = placed.tile([P, 2, PACK, BANK], BF16, name="h_tiles1_0", align_bytes=256, offset=LATE)[:, 0]
         h_packed = {
-            (0, 0): placed.tile([P, BANK * PACK], BF16, name="h_packed0_0", align_bytes=64, offset=T * BYTES + 2048),
+            (0, 0): placed.tile([P, BANK * PACK], BF16, name="h_packed0_0", align_bytes=256, offset=T * BYTES + 2048),
             (1, 0): sbuf("h_packed1_0", [P, BANK * PACK], BF16),
         }
         h_codes = {b: sbuf("h_codes%d_%d" % b, [P, BANK], U32) for b in blocks}
@@ -260,14 +254,13 @@ def tile_list_listed_click_probabilities_kernel(
                         layer_pass(group0[half][t], 0, t, half, a, a == 1, False)
             if a == 0:
                 reorder_columns(w4_plane[:], w4_plane_raw[:].rearrange("p a c -> p (a c)").bitcast(U8), 16)
-                for first in (0, S2 // 2):
-                    nc.vector.tensor_copy(
-                        item_plane[:].bitcast(U8)[:, first : first + S2 // 2],
-                        item_rows[:].bitcast(U8).indirect(entries(items, first, S2 // 2)),
-                    )
+                nc.vector.tensor_copy(item_picked[:].bitcast(U8), item_rows[:].bitcast(U8).indirect(items[:]))
         for a in range(GROUPS):
-            item_table.append(placed.tile([P, T2], I32, name="item_table%d" % a, align_bytes=64, offset=a * T2 * BYTES))
+            item_table.append(placed.tile([P, T2], I32, name="item_table%d" % a, align_bytes=256, offset=a * T2 * BYTES))
             nc.sync.dma_start(item_table[a][:], tab2_words[a].rearrange("p t i -> p (t i)").bitcast(I32))
+        for a in range(GROUPS):
+            for r in range(ROWS):
+                nc.sync.dma_start(item_plane[ITEM_SHIFT + ROWS * a + r : P : QUAD, :], item_picked[64 * a + 4 * r : 64 * (a + 1) : 16, :])
         round_w1(0, nc.scalar.copy, slice(0, SCALAR_SHARE))
         round_w1(0, nc.vector.tensor_copy, slice(SCALAR_SHARE, P))
         quantize_w1(0, slice(0, 1))
@@ -317,14 +310,14 @@ def tile_list_listed_click_probabilities_kernel(
 
         def gather_late(g, chunk):
             words = placed.tile(
-                [P, ITEM_CHUNK], U32, name="item_words%d_%d" % (g, chunk), align_bytes=64, offset=LATE + (len(item_words) - 3) * ITEM_CHUNK * BYTES
+                [P, ITEM_CHUNK], U32, name="item_words%d_%d" % (g, chunk), align_bytes=256, offset=LATE + (len(item_words) - 3) * ITEM_CHUNK * BYTES
             )
             item_words[g, chunk] = words[:]
             gather_items(words[:], g, chunk * ITEM_CHUNK, ITEM_CHUNK)
 
         def score(sums, tiles, half, columns):
             count = columns.stop - columns.start
-            prob = results.tile([P, len(tiles), count], F32, name="prob")
+            prob = results.tile([P, len(tiles), count], F32, name="prob", align_bytes=256)
             for n, i in enumerate(tiles):
                 part = max(c for c, (first, size) in enumerate(item_chunks) if first <= i * P)
                 at = i * P - item_chunks[part][0]
@@ -347,7 +340,7 @@ def tile_list_listed_click_probabilities_kernel(
 
         whole = slice(0, BANK)
         gather_items(early_items[:], 0, 0, 2 * ITEM_CHUNK)
-        first_items = placed.tile([P, ITEM_CHUNK], U32, name="first_items", align_bytes=64, offset=T * BYTES + 2048)
+        first_items = placed.tile([P, ITEM_CHUNK], U32, name="first_items", align_bytes=256, offset=T * BYTES + 2048)
         item_words[1, 0] = first_items[:]
         gather_items(first_items[:], 1, 0, ITEM_CHUNK)
         quantize_h(1, 0)
@@ -363,7 +356,7 @@ def tile_list_listed_click_probabilities_kernel(
                 last_sum = bank(0)
                 open_group1(last_sum, PACK - 1, 1)
                 close_group1(last_sum, PACK - 1, 1)
-        h_packed[0, 1] = placed.tile([P, BANK * PACK], BF16, name="h_packed0_1", align_bytes=64, offset=0)
+        h_packed[0, 1] = placed.tile([P, BANK * PACK], BF16, name="h_packed0_1", align_bytes=256, offset=0)
         h_packed[1, 1] = sbuf("h_packed1_1", [P, BANK * PACK], BF16)
         sums = [bank(i) for i in range(ITEM_TILES)]
         for s in range(PIECES):

@@ -49,7 +49,7 @@ def tile_list_listed_click_probabilities_kernel(
     with ExitStack() as ctx:
         lists = ctx.enter_context(tc.tile_pool(name="lists", bufs=1))
         keep = ctx.enter_context(tc.tile_pool(name="keep", bufs=1))
-        results = ctx.enter_context(tc.tile_pool(name="results", bufs=13))
+        results = ctx.enter_context(tc.tile_pool(name="results", bufs=14))
         placed = ctx.enter_context(tc.tile_pool(name="placed", bufs=1))
         psum = ctx.enter_context(tc.psum_pool(name="psum", bufs=1))
 
@@ -81,18 +81,15 @@ def tile_list_listed_click_probabilities_kernel(
         item_plane = sbuf("item_plane", [P, S2 // BYTES], I32)
         nc.vector.memset(item_plane[:], 0)
 
+        warm = sbuf("warm", [P, 2], F32)
+        nc.vector.memset(warm[:], 0.0)
+        nc.scalar.activation(warm[:, 1:2], warm[:, 0:1], ACT.Sigmoid)
+
         w4_view = w4_words.rearrange("a p c -> p a c").bitcast(I32)
         w4_span = 2 * K_PASS // BYTES
         w4_raw = [sbuf("w4_raw0", [P, W4_PASSES, w4_span], I32)]
-        nc.sync.dma_start(w4_raw[0][:], w4_view[:, :, 0:w4_span])
-        nc.sync.dma_start(users[:], offs)
-        nc.sync.dma_start(items[:], offs2)
         b1_cols = sbuf("b1_cols", [P, GROUPS, PACK], F32)
-        nc.sync.dma_start(b1_cols[:], b1.rearrange("(g p t) -> p g t", p=P, t=PACK))
-        nc.sync.dma_start(user_rows[0:P:4, :], tab_scales[1:3].rearrange("a q t -> (a q) t").bitcast(I32))
-        nc.sync.dma_start(user_rows[6:P:8, :], tab_scales[0].bitcast(I32))
         w1_rows = w1.rearrange("(p j) c -> p j c", j=PACK)
-        nc.sync.dma_start(b2_rows[0:ITEM_TILES, :], b2.rearrange("(i p) -> i p", p=P))
         user_table = [
             sbuf("user_table0", [P, T], I32, "shared_a"),
             sbuf("user_table1", [P, T], I32, "shared_e"),
@@ -103,13 +100,20 @@ def tile_list_listed_click_probabilities_kernel(
             nc.sync.dma_start(user_table[a][:, columns], tab_words[a].rearrange("p t i -> p (t i)").bitcast(I32)[:, columns])
 
         load_user_pass(0, slice(0, T // 2))
+        nc.sync.dma_start(users[:], offs)
+        nc.sync.dma_start(user_rows[0:P:4, :], tab_scales[1:3].rearrange("a q t -> (a q) t").bitcast(I32))
+        nc.sync.dma_start(user_rows[6:P:8, :], tab_scales[0].bitcast(I32))
+        nc.sync.dma_start(w4_raw[0][:], w4_view[:, :, 0:w4_span])
+        nc.sync.dma_start(item_rows[0:P:4, :], tab2_scales.rearrange("a q t -> (a q) t").bitcast(I32))
+        nc.sync.dma_start(items[:], offs2)
+        load_user_pass(0, slice(T // 2, T))
         for r in range(ROWS):
             nc.sync.dma_start(
                 w4_plane_raw[r:P:QUAD, :, :],
                 w4_scales[:, r : P // 8 : ROWS, :].rearrange("a q c -> q a c").bitcast(I32),
             )
-        load_user_pass(0, slice(T // 2, T))
-        nc.sync.dma_start(item_rows[0:P:4, :], tab2_scales.rearrange("a q t -> (a q) t").bitcast(I32))
+        nc.sync.dma_start(b1_cols[:], b1.rearrange("(g p t) -> p g t", p=P, t=PACK))
+        nc.sync.dma_start(b2_rows[0:ITEM_TILES, :], b2.rearrange("(i p) -> i p", p=P))
 
         identity = sbuf("identity", [P, P], F32)
         make_identity(nc, identity[:])
@@ -299,7 +303,7 @@ def tile_list_listed_click_probabilities_kernel(
         early_items = sbuf("early_items", [P, 2 * ITEM_CHUNK], U32, "shared_h")
         item_words = {(0, chunk): early_items[:, chunk * ITEM_CHUNK : (chunk + 1) * ITEM_CHUNK] for chunk in range(2)}
         sums = [bank(PACK + t) for t in range(PACK)]
-        for t in range(PACK - 1):
+        for t in range(PACK):
             open_group1(sums[t], t, 1)
             close_group1(sums[t], t, 1)
 
@@ -352,10 +356,6 @@ def tile_list_listed_click_probabilities_kernel(
             sums = {i: bank(i) for i in tiles}
             for pair in ([[0], [1]] if chunk == 0 else in_pairs(tiles)):
                 score(sums, pair, 0, whole)
-            if chunk == 0:
-                last_sum = bank(0)
-                open_group1(last_sum, PACK - 1, 1)
-                close_group1(last_sum, PACK - 1, 1)
         h_packed[0, 1] = placed.tile([P, BANK * PACK], BF16, name="h_packed0_1", align_bytes=256, offset=0)
         h_packed[1, 1] = sbuf("h_packed1_1", [P, BANK * PACK], BF16)
         sums = [bank(i) for i in range(ITEM_TILES)]
@@ -367,7 +367,7 @@ def tile_list_listed_click_probabilities_kernel(
             if s == 0:
                 for pair in in_pairs(list(range(SPLIT_TILES))):
                     score(sums, pair, 1, slice(0, width))
-        for pair in in_pairs(list(range(SPLIT_TILES, ITEM_TILES))):
-            score(sums, pair, 1, whole)
-        for pair in in_pairs(list(range(SPLIT_TILES))):
+        for i in range(SPLIT_TILES, ITEM_TILES):
+            score(sums, [i], 1, whole)
+        for pair in in_pairs(list(range(SPLIT_TILES - 2))) + [[SPLIT_TILES - 2], [SPLIT_TILES - 1]]:
             score(sums, pair, 1, slice(width, BANK))

@@ -38,6 +38,7 @@ ITEM_SHIFT = 8
 MOVES_AHEAD = 6
 SPLIT_TILES = 6
 LATE = 2 * T * BYTES + 2048
+FIRST_COLUMNS = 3 * T // 8
 SCALAR_SHARE = 56
 PIECES = 2
 
@@ -69,13 +70,13 @@ def tile_list_listed_click_probabilities_kernel(
         user_plane = [sbuf("user_plane%d" % a, [P, S // BYTES], I32) for a in range(USER_PASSES)]
         w4_plane_raw = sbuf("w4_plane_raw", [P, W4_PASSES, H // BYTES], I32, "shared_d")
         item_rows = sbuf("item_rows", [P, T2 // BYTES], I32, "shared_f")
-        b2_rows = sbuf("b2_rows", [P, P], F32)
+        bias_rows = sbuf("bias_rows", [P, K_PASS], F32)
         middle = T // BYTES // 2
         nc.gpsimd.memset(user_rows[:, :middle], 0)
-        nc.gpsimd.memset(b2_rows[:], 0.0)
         nc.vector.memset(user_rows[:, middle:], 0)
-        nc.vector.memset(w4_plane_raw[:], 0)
         nc.vector.memset(item_rows[:], 0)
+        nc.vector.memset(w4_plane_raw[:], 0)
+        nc.vector.memset(bias_rows[:], 0.0)
         for a in range(USER_PASSES):
             nc.vector.memset(user_plane[a][:], 0)
         item_plane = sbuf("item_plane", [P, S2 // BYTES], I32)
@@ -99,26 +100,30 @@ def tile_list_listed_click_probabilities_kernel(
         def load_user_pass(a, columns=slice(0, T)):
             nc.sync.dma_start(user_table[a][:, columns], tab_words[a].rearrange("p t i -> p (t i)").bitcast(I32)[:, columns])
 
-        load_user_pass(0, slice(0, T // 2))
+        load_user_pass(0, slice(0, FIRST_COLUMNS))
         nc.sync.dma_start(users[:], offs)
         nc.sync.dma_start(user_rows[0:P:4, :], tab_scales[1:3].rearrange("a q t -> (a q) t").bitcast(I32))
         nc.sync.dma_start(user_rows[6:P:8, :], tab_scales[0].bitcast(I32))
         nc.sync.dma_start(w4_raw[0][:], w4_view[:, :, 0:w4_span])
         nc.sync.dma_start(item_rows[0:P:4, :], tab2_scales.rearrange("a q t -> (a q) t").bitcast(I32))
         nc.sync.dma_start(items[:], offs2)
-        load_user_pass(0, slice(T // 2, T))
+        load_user_pass(0, slice(FIRST_COLUMNS, T))
         for r in range(ROWS):
             nc.sync.dma_start(
                 w4_plane_raw[r:P:QUAD, :, :],
                 w4_scales[:, r : P // 8 : ROWS, :].rearrange("a q c -> q a c").bitcast(I32),
             )
-        nc.sync.dma_start(b1_cols[:], b1.rearrange("(g p t) -> p g t", p=P, t=PACK))
-        nc.sync.dma_start(b2_rows[0:ITEM_TILES, :], b2.rearrange("(i p) -> i p", p=P))
+        nc.sync.dma_start(bias_rows[0:ITEM_TILES, 0:P], b2.rearrange("(i p) -> i p", p=P))
+        nc.sync.dma_start(bias_rows[ITEM_TILES : ITEM_TILES + GROUPS, :], b1.rearrange("(g c) -> g c", c=K_PASS))
 
         identity = sbuf("identity", [P, P], F32)
         make_identity(nc, identity[:])
         b2_turned = bank(BANKS - 1, P)
-        nc.tensor.transpose(b2_turned[:], b2_rows[:], identity[:])
+        nc.tensor.transpose(b2_turned[:], bias_rows[:, 0:P], identity[:])
+        b1_turned = bank(BANKS - 2)
+        for t in range(PACK):
+            nc.tensor.transpose(b1_turned[:, t * P : (t + 1) * P], bias_rows[:, t:K_PASS:PACK], identity[:])
+        nc.scalar.copy(b1_cols[:], b1_turned[:].rearrange("p (t row) -> p row t", t=PACK)[:, ITEM_TILES : ITEM_TILES + GROUPS, :])
         b2_cols = sbuf("b2_cols", [P, ITEM_TILES], F32)
         nc.scalar.copy(b2_cols[:], b2_turned[:, 0:ITEM_TILES])
 

@@ -73,10 +73,10 @@ def tile_list_listed_click_probabilities_kernel(
         bias_rows = sbuf("bias_rows", [P, K_PASS], F32)
         middle = T // BYTES // 2
         nc.gpsimd.memset(user_rows[:, :middle], 0)
+        nc.gpsimd.memset(bias_rows[:], 0.0)
         nc.vector.memset(user_rows[:, middle:], 0)
         nc.vector.memset(item_rows[:], 0)
         nc.vector.memset(w4_plane_raw[:], 0)
-        nc.vector.memset(bias_rows[:], 0.0)
         for a in range(USER_PASSES):
             nc.vector.memset(user_plane[a][:], 0)
         item_plane = sbuf("item_plane", [P, S2 // BYTES], I32)
@@ -104,16 +104,16 @@ def tile_list_listed_click_probabilities_kernel(
         nc.sync.dma_start(users[:], offs)
         nc.sync.dma_start(user_rows[0:P:4, :], tab_scales[1:3].rearrange("a q t -> (a q) t").bitcast(I32))
         nc.sync.dma_start(user_rows[6:P:8, :], tab_scales[0].bitcast(I32))
-        nc.sync.dma_start(w4_raw[0][:], w4_view[:, :, 0:w4_span])
         nc.sync.dma_start(item_rows[0:P:4, :], tab2_scales.rearrange("a q t -> (a q) t").bitcast(I32))
         nc.sync.dma_start(items[:], offs2)
+        nc.sync.dma_start(bias_rows[0:ITEM_TILES, 0:P], b2.rearrange("(i p) -> i p", p=P))
         load_user_pass(0, slice(FIRST_COLUMNS, T))
+        nc.sync.dma_start(w4_raw[0][:], w4_view[:, :, 0:w4_span])
         for r in range(ROWS):
             nc.sync.dma_start(
                 w4_plane_raw[r:P:QUAD, :, :],
                 w4_scales[:, r : P // 8 : ROWS, :].rearrange("a q c -> q a c").bitcast(I32),
             )
-        nc.sync.dma_start(bias_rows[0:ITEM_TILES, 0:P], b2.rearrange("(i p) -> i p", p=P))
         nc.sync.dma_start(bias_rows[ITEM_TILES : ITEM_TILES + GROUPS, :], b1.rearrange("(g c) -> g c", c=K_PASS))
 
         identity = sbuf("identity", [P, P], F32)
@@ -174,8 +174,8 @@ def tile_list_listed_click_probabilities_kernel(
         def round_w1(run, copy, share):
             g, at = divmod(w1_runs[run][0], K_PASS)
             copy(
-                w1_bf16[g][:].rearrange("p (t m j) -> p m t j", t=PACK, j=PACK)[:, at // PACK + share.start : at // PACK + share.stop],
-                w1_run(run).rearrange("p j (m t) -> p m t j", t=PACK)[:, share],
+                w1_bf16[g][:].rearrange("p (t m u j) -> p m u t j", t=PACK, u=2, j=2)[:, at // PACK + share.start : at // PACK + share.stop],
+                w1_run(run).rearrange("p (u j) (m t) -> p m u t j", t=PACK, u=2)[:, share],
             )
 
         def quantize_w1(g, tiles):

@@ -67,7 +67,9 @@ def tile_list_listed_click_probabilities_kernel(
         items = lists.tile([P, S2 // PER_COLUMN], U16, name="items")
 
         user_rows = placed.tile([P, T // BYTES], I32, name="user_rows", align_bytes=256, offset=T * BYTES - T // 4)
-        user_plane = [sbuf("user_plane%d" % a, [P, S // BYTES], I32) for a in range(USER_PASSES)]
+        w4_user_planes = sbuf("w4_user_planes", [P, W4_PASSES, S // BYTES], I32)
+        w1_user_plane = sbuf("w1_user_plane", [P, S // BYTES], I32)
+        user_plane = [w1_user_plane[:]] + [w4_user_planes[:, a, :] for a in range(W4_PASSES)]
         w4_plane_raw = sbuf("w4_plane_raw", [P, W4_PASSES, H // BYTES], I32, "shared_d")
         item_rows = sbuf("item_rows", [P, T2 // BYTES], I32, "shared_f")
         bias_rows = sbuf("bias_rows", [P, K_PASS], F32)
@@ -77,9 +79,9 @@ def tile_list_listed_click_probabilities_kernel(
         nc.vector.memset(user_rows[:, middle:], 0)
         nc.vector.memset(item_rows[:], 0)
         nc.vector.memset(w4_plane_raw[:], 0)
-        for a in range(USER_PASSES):
-            nc.vector.memset(user_plane[a][:], 0)
-        item_plane = sbuf("item_plane", [P, S2 // BYTES], I32)
+        nc.vector.memset(w4_user_planes[:], 0)
+        nc.vector.memset(w1_user_plane[:], 0)
+        item_plane = sbuf("item_plane", [P, GROUPS, S2 // BYTES], I32)
         nc.vector.memset(item_plane[:], 0)
 
         warm = sbuf("warm", [P, 2], F32)
@@ -102,9 +104,9 @@ def tile_list_listed_click_probabilities_kernel(
 
         load_user_pass(0, slice(0, FIRST_COLUMNS))
         nc.sync.dma_start(users[:], offs)
-        nc.sync.dma_start(user_rows[0:P:4, :], tab_scales[1:3].rearrange("a q t -> (a q) t").bitcast(I32))
+        nc.sync.dma_start(user_rows[0:P:4, :], tab_scales[1:3].rearrange("a q t -> q a t").bitcast(I32))
         nc.sync.dma_start(user_rows[6:P:8, :], tab_scales[0].bitcast(I32))
-        nc.sync.dma_start(item_rows[0:P:4, :], tab2_scales.rearrange("a q t -> (a q) t").bitcast(I32))
+        nc.sync.dma_start(item_rows[0:P:4, :], tab2_scales.rearrange("a q t -> q a t").bitcast(I32))
         nc.sync.dma_start(items[:], offs2)
         nc.sync.dma_start(bias_rows[0:ITEM_TILES, 0:P], b2.rearrange("(i p) -> i p", p=P))
         load_user_pass(0, slice(FIRST_COLUMNS, T))
@@ -131,10 +133,8 @@ def tile_list_listed_click_probabilities_kernel(
 
         user_picked = sbuf("user_picked", [P, S // BYTES], I32)
         nc.vector.tensor_copy(user_picked[:].bitcast(U8), user_rows[:].bitcast(U8).indirect(users[:]))
-        moves = []
-        for a in range(1, USER_PASSES):
-            moves += [(user_plane[a][r:P:QUAD, :], user_picked[64 * (a - 1) + 4 * r : 64 * a : 16, :]) for r in range(ROWS)]
-        moves += [(user_plane[0][ROWS + r : P : QUAD, :], user_picked[6 + 8 * r : P : 32, :]) for r in range(ROWS)]
+        moves = [(w4_user_planes[q : q + ROWS, :, :], user_picked[q : q + QUAD : 4, :]) for q in range(0, P, QUAD)]
+        moves += [(w1_user_plane[q + ROWS : q + 2 * ROWS, :], user_picked[q + 6 : q + QUAD : 8, :]) for q in range(0, P, QUAD)]
         for destination, source in moves[:MOVES_AHEAD]:
             nc.sync.dma_start(destination, source)
         load_user_pass(2)
@@ -267,9 +267,8 @@ def tile_list_listed_click_probabilities_kernel(
         for a in range(GROUPS):
             item_table.append(placed.tile([P, T2], I32, name="item_table%d" % a, align_bytes=256, offset=a * T2 * BYTES))
             nc.sync.dma_start(item_table[a][:], tab2_words[a].rearrange("p t i -> p (t i)").bitcast(I32))
-        for a in range(GROUPS):
-            for r in range(ROWS):
-                nc.sync.dma_start(item_plane[ITEM_SHIFT + ROWS * a + r : P : QUAD, :], item_picked[64 * a + 4 * r : 64 * (a + 1) : 16, :])
+        for q in range(0, P, QUAD):
+            nc.sync.dma_start(item_plane[q + ITEM_SHIFT : q + ITEM_SHIFT + ROWS, :, :], item_picked[q : q + QUAD : 4, :])
         round_w1(0, nc.scalar.copy, slice(0, SCALAR_SHARE))
         round_w1(0, nc.vector.tensor_copy, slice(SCALAR_SHARE, P))
         quantize_w1(0, slice(0, 1))
@@ -334,7 +333,7 @@ def tile_list_listed_click_probabilities_kernel(
                     nc.tensor.matmul_mx(
                         out=sums[i][:, columns],
                         lhsT=item_words[g, part][:, at : at + P].bitcast(FP8X4),
-                        lhsT_scale=item_plane[ITEM_SHIFT + ROWS * g : P, :].bitcast(U8)[:, i * P : (i + 1) * P],
+                        lhsT_scale=item_plane[ITEM_SHIFT:P, g, :].bitcast(U8)[:, i * P : (i + 1) * P],
                         rhs=h_codes[g, half][:, columns].bitcast(FP8X4),
                         rhs_scale=h_plane[g, half][:, columns],
                         start=g == 0,

from contextlib import ExitStack

import concourse.mybir as mybir
from concourse.masks import make_identity

K1, K2, H = 512, 1024, 1024
T, S = 4096, 1024
T2, S2 = 2048, 1024
FLOPS = 2 * (K1 + K2) * H * S + 2 * H * S2 * S

F32 = mybir.dt.float32
BF16 = mybir.dt.bfloat16
I32 = mybir.dt.int32
U32 = mybir.dt.uint32
U16 = mybir.dt.uint16
U8 = mybir.dt.uint8
FP8X4 = mybir.dt.float8_e4m3fn_x4
FP4X4 = mybir.dt.float4_e2m1fn_x4
ACT = mybir.ActivationFunctionType
ALU = mybir.AluOpType

P = 128
PACK = 4
K_PASS = P * PACK
QUAD = 32
ROWS = 4
BYTES = 4
PER_COLUMN = 16
BANK = 512
BANKS = 8
HALVES = S // BANK
USER_PASSES = (K1 + K2) // K_PASS
W4_PASSES = K2 // K_PASS
GROUPS = H // K_PASS
ITEM_TILES = S2 // P
ITEM_CHUNK = 2 * P
ITEM_SHIFT = 8
MOVES_AHEAD = 6
SPLIT_TILES = 6
LATE = 2 * T * BYTES + 2048
FIRST_COLUMNS = 3 * T // 8
SCALAR_SHARE = 56
PIECES = 2


def tile_list_listed_click_probabilities_kernel(
    tc, tab_words, tab_scales, offs, tab2_words, tab2_scales, offs2, w1, w4_words, w4_scales, b1, b2, out
):
    nc = tc.nc
    with ExitStack() as ctx:
        lists = ctx.enter_context(tc.tile_pool(name="lists", bufs=1))
        keep = ctx.enter_context(tc.tile_pool(name="keep", bufs=1))
        results = ctx.enter_context(tc.tile_pool(name="results", bufs=14))
        placed = ctx.enter_context(tc.tile_pool(name="placed", bufs=1))
        psum = ctx.enter_context(tc.psum_pool(name="psum", bufs=1))

        def sbuf(name, shape, dtype, tag=None):
            return keep.tile(shape, dtype, name=name, tag=tag or name, align_bytes=256)

        def bank(b, columns=BANK):
            return psum.tile([P, columns], F32, name="bank%d" % b)

        def entries(listed, first, count):
            return listed[:, first // PER_COLUMN : (first + count) // PER_COLUMN]

        users = lists.tile([P, S // PER_COLUMN], U16, name="users")
        items = lists.tile([P, S2 // PER_COLUMN], U16, name="items")

        user_rows = placed.tile([P, T // BYTES], I32, name="user_rows", align_bytes=256, offset=T * BYTES - T // 4)
        w4_user_planes = sbuf("w4_user_planes", [P, W4_PASSES, S // BYTES], I32)
        w1_user_plane = sbuf("w1_user_plane", [P, S // BYTES], I32)
        user_plane = [w1_user_plane[:]] + [w4_user_planes[:, a, :] for a in range(W4_PASSES)]
        w4_plane_raw = sbuf("w4_plane_raw", [P, W4_PASSES, H // BYTES], I32, "shared_d")
        item_rows = sbuf("item_rows", [P, T2 // BYTES], I32, "shared_f")
        bias_rows = sbuf("bias_rows", [P, K_PASS], F32)
        middle = T // BYTES // 2
        nc.gpsimd.memset(user_rows[:, :middle], 0)
        nc.gpsimd.memset(bias_rows[:], 0.0)
        nc.vector.memset(user_rows[:, middle:], 0)
        nc.vector.memset(item_rows[:], 0)
        nc.vector.memset(w4_plane_raw[:], 0)
        nc.vector.memset(w4_user_planes[:], 0)
        nc.vector.memset(w1_user_plane[:], 0)
        item_plane = sbuf("item_plane", [P, GROUPS, S2 // BYTES], I32)
        nc.vector.memset(item_plane[:], 0)

        warm = sbuf("warm", [P, 2], F32)
        nc.vector.memset(warm[:], 0.0)
        nc.scalar.activation(warm[:, 1:2], warm[:, 0:1], ACT.Sigmoid)

        w4_view = w4_words.rearrange("a p c -> p a c").bitcast(I32)
        w4_span = 2 * K_PASS // BYTES
        w4_raw = [sbuf("w4_raw0", [P, W4_PASSES, w4_span], I32)]
        b1_cols = sbuf("b1_cols", [P, GROUPS, PACK], F32)
        w1_rows = w1.rearrange("(p j) c -> p j c", j=PACK)
        user_table = [
            sbuf("user_table0", [P, T], I32, "shared_a"),
            sbuf("user_table1", [P, T], I32, "shared_e"),
            placed.tile([P, T], I32, name="user_table2", align_bytes=256, offset=0),
        ]

        def load_user_pass(a, columns=slice(0, T)):
            nc.sync.dma_start(user_table[a][:, columns], tab_words[a].rearrange("p t i -> p (t i)").bitcast(I32)[:, columns])

        load_user_pass(0, slice(0, FIRST_COLUMNS))
        nc.sync.dma_start(users[:], offs)
        nc.sync.dma_start(user_rows[0:P:4, :], tab_scales[1:3].rearrange("a q t -> q a t").bitcast(I32))
        nc.sync.dma_start(user_rows[6:P:8, :], tab_scales[0].bitcast(I32))
        nc.sync.dma_start(item_rows[0:P:4, :], tab2_scales.rearrange("a q t -> q a t").bitcast(I32))
        nc.sync.dma_start(items[:], offs2)
        nc.sync.dma_start(bias_rows[0:ITEM_TILES, 0:P], b2.rearrange("(i p) -> i p", p=P))
        load_user_pass(0, slice(FIRST_COLUMNS, T))
        nc.sync.dma_start(w4_raw[0][:], w4_view[:, :, 0:w4_span])
        for r in range(ROWS):
            nc.sync.dma_start(
                w4_plane_raw[r:P:QUAD, :, :],
                w4_scales[:, r : P // 8 : ROWS, :].rearrange("a q c -> q a c").bitcast(I32),
            )
        nc.sync.dma_start(bias_rows[ITEM_TILES : ITEM_TILES + GROUPS, :], b1.rearrange("(g c) -> g c", c=K_PASS))

        identity = sbuf("identity", [P, P], F32)
        make_identity(nc, identity[:])
        b2_turned = bank(BANKS - 1, P)
        nc.tensor.transpose(b2_turned[:], bias_rows[:, 0:P], identity[:])
        b1_turned = bank(BANKS - 2)
        for t in range(PACK):
            nc.tensor.transpose(b1_turned[:, t * P : (t + 1) * P], bias_rows[:, t:K_PASS:PACK], identity[:])
        nc.scalar.copy(b1_cols[:], b1_turned[:].rearrange("p (t row) -> p row t", t=PACK)[:, ITEM_TILES : ITEM_TILES + GROUPS, :])
        b2_cols = sbuf("b2_cols", [P, ITEM_TILES], F32)
        nc.scalar.copy(b2_cols[:], b2_turned[:, 0:ITEM_TILES])

        load_user_pass(1)

        user_picked = sbuf("user_picked", [P, S // BYTES], I32)
        nc.vector.tensor_copy(user_picked[:].bitcast(U8), user_rows[:].bitcast(U8).indirect(users[:]))
        moves = [(w4_user_planes[q : q + ROWS, :, :], user_picked[q : q + QUAD : 4, :]) for q in range(0, P, QUAD)]
        moves += [(w1_user_plane[q + ROWS : q + 2 * ROWS, :], user_picked[q + 6 : q + QUAD : 8, :]) for q in range(0, P, QUAD)]
        for destination, source in moves[:MOVES_AHEAD]:
            nc.sync.dma_start(destination, source)
        load_user_pass(2)
        for destination, source in moves[MOVES_AHEAD:]:
            nc.sync.dma_start(destination, source)

        def reorder_columns(ordered, raw, line):
            nc.vector.tensor_copy(
                ordered.rearrange("p (b t c i) -> p b c t i", t=PACK, c=P // line, i=line),
                raw.rearrange("p (b c i t) -> p b c t i", t=PACK, c=P // line, i=line),
            )

        w4_codes = [sbuf("w4_codes%d" % g, [P, W4_PASSES * 2 * K_PASS], U8) for g in range(GROUPS)]
        w4_plane = sbuf("w4_plane", [P, W4_PASSES * H], U8)

        def reorder_w4(g):
            reorder_columns(w4_codes[g][:].bitcast(U16), w4_raw[g][:].rearrange("p a c -> p (a c)").bitcast(U16), 8)

        reorder_w4(0)

        w4_raw.append(placed.tile([P, W4_PASSES, w4_span], I32, name="w4_raw1", align_bytes=256, offset=T * BYTES))
        w1_raw = placed.tile([P, PACK * H], F32, name="w1_raw", align_bytes=256, offset=T * BYTES + 2048)
        w1_runs = [(0, K_PASS), (K_PASS, K_PASS // 2), (3 * K_PASS // 2, K_PASS // 2)]

        def w1_run(run):
            first, count = w1_runs[run]
            return w1_raw[:, PACK * first : PACK * (first + count)].rearrange("p (j c) -> p j c", j=PACK)

        for run, (first, count) in enumerate(w1_runs):
            if run == 1:
                nc.sync.dma_start(w4_raw[1][:], w4_view[:, :, w4_span : 2 * w4_span])
            nc.sync.dma_start(w1_run(run), w1_rows[:, :, first : first + count])
        w1_bf16 = [sbuf("w1_bf16_%d" % g, [P, PACK * K_PASS], BF16) for g in range(GROUPS)]
        w1_codes = [sbuf("w1_codes%d" % g, [P, K_PASS], U32) for g in range(GROUPS)]
        w1_plane = [sbuf("w1_plane%d" % g, [P, K_PASS], U8) for g in range(GROUPS)]

        def round_w1(run, copy, share):
            g, at = divmod(w1_runs[run][0], K_PASS)
            copy(
                w1_bf16[g][:].rearrange("p (t m u j) -> p m u t j", t=PACK, u=2, j=2)[:, at // PACK + share.start : at // PACK + share.stop],
                w1_run(run).rearrange("p (u j) (m t) -> p m u t j", t=PACK, u=2)[:, share],
            )

        def quantize_w1(g, tiles):
            columns = slice(tiles.start * P, tiles.stop * P)
            nc.vector.quantize_mx(
                out=w1_codes[g][:, columns].bitcast(FP8X4),
                scales=w1_plane[g][:, columns],
                in_=w1_bf16[g][:, PACK * columns.start : PACK * columns.stop],
            )

        item_picked = sbuf("item_picked", [P, S2 // BYTES], I32)

        user_words = {}
        user_words_tag = {(1, 0): "shared_d", (2, 0): "shared_f"}

        def gather_users(a, half):
            user_words[a, half] = sbuf("user_words%d_%d" % (a, half), [P, BANK], U32, user_words_tag.get((a, half)))
            window = user_table[a][:].bitcast(U32)
            nc.vector.tensor_copy(user_words[a, half][:], window.indirect(entries(users, half * BANK, BANK)))

        def layer_pass(acc, g, t, half, a, start, stop):
            if a == 0:
                columns = slice(t * P, (t + 1) * P)
                weights, weight_scales = w1_codes[g][:, columns].bitcast(FP8X4), w1_plane[g][:, columns]
            else:
                first = (a - 1) * H + (g * PACK + t) * P
                at = (a - 1) * K_PASS + t * P
                weights = w4_codes[g][:, 2 * at : 2 * (at + P)].bitcast(FP4X4)
                weight_scales = w4_plane[:, first : first + P]
            nc.tensor.matmul_mx(
                out=acc[:],
                lhsT=weights,
                lhsT_scale=weight_scales,
                rhs=user_words[a, half][:].bitcast(FP8X4),
                rhs_scale=user_plane[a][ROWS if a == 0 else 0 : P, :].bitcast(U8)[:, half * BANK : (half + 1) * BANK],
                start=start,
                stop=stop,
            )

        blocks = [(g, half) for g in range(GROUPS) for half in range(HALVES)]
        h_tiles = {b: sbuf("h_tiles%d_%d" % b, [P, PACK, BANK], BF16, "shared_h" if b == (0, 0) else None) for b in blocks if b != (1, 0)}
        h_tiles[1, 0] = placed.tile([P, 2, PACK, BANK], BF16, name="h_tiles1_0", align_bytes=256, offset=LATE)[:, 0]
        h_packed = {
            (0, 0): placed.tile([P, BANK * PACK], BF16, name="h_packed0_0", align_bytes=256, offset=T * BYTES + 2048),
            (1, 0): sbuf("h_packed1_0", [P, BANK * PACK], BF16),
        }
        h_codes = {b: sbuf("h_codes%d_%d" % b, [P, BANK], U32) for b in blocks}
        h_plane = {b: sbuf("h_plane%d_%d" % b, [P, BANK], U8) for b in blocks}

        def relu_out(acc, g, t, half):
            bias = b1_cols[:, g, t : t + 1]
            if (g, half, t) == (0, 0, PACK - 1):
                nc.vector.tensor_scalar(h_tiles[g, half][:, t, :], acc[:], bias, 0.0, ALU.add, ALU.max)
            else:
                nc.scalar.activation(h_tiles[g, half][:, t, :], acc[:], ACT.Relu, bias=bias)

        width = BANK // PIECES

        def interleave_h(g, half, s):
            nc.vector.tensor_copy(
                h_packed[g, half][:, s * width * PACK : (s + 1) * width * PACK].rearrange("p (c i t) -> p c t i", i=4, t=PACK),
                h_tiles[g, half][:, :, s * width : (s + 1) * width].rearrange("p t (c i) -> p c t i", i=4),
            )

        def quantize_piece(g, half, s):
            nc.vector.quantize_mx(
                out=h_codes[g, half][:, s * width : (s + 1) * width].bitcast(FP8X4),
                scales=h_plane[g, half][:, s * width : (s + 1) * width],
                in_=h_packed[g, half][:, s * width * PACK : (s + 1) * width * PACK],
            )

        def quantize_h(g, half):
            for s in range(PIECES):
                interleave_h(g, half, s)
            for s in range(PIECES):
                quantize_piece(g, half, s)

        item_table = []
        group0 = [[bank(PACK * half + t) for t in range(PACK)] for half in range(HALVES)]
        for a in range(USER_PASSES):
            for half in range(HALVES):
                gather_users(a, half)
                if a > 0:
                    for t in range(PACK):
                        layer_pass(group0[half][t], 0, t, half, a, a == 1, False)
            if a == 0:
                reorder_columns(w4_plane[:], w4_plane_raw[:].rearrange("p a c -> p (a c)").bitcast(U8), 16)
                nc.vector.tensor_copy(item_picked[:].bitcast(U8), item_rows[:].bitcast(U8).indirect(items[:]))
        for a in range(GROUPS):
            item_table.append(placed.tile([P, T2], I32, name="item_table%d" % a, align_bytes=256, offset=a * T2 * BYTES))
            nc.sync.dma_start(item_table[a][:], tab2_words[a].rearrange("p t i -> p (t i)").bitcast(I32))
        for q in range(0, P, QUAD):
            nc.sync.dma_start(item_plane[q + ITEM_SHIFT : q + ITEM_SHIFT + ROWS, :, :], item_picked[q : q + QUAD : 4, :])
        round_w1(0, nc.scalar.copy, slice(0, SCALAR_SHARE))
        round_w1(0, nc.vector.tensor_copy, slice(SCALAR_SHARE, P))
        quantize_w1(0, slice(0, 1))
        quantize_w1(0, slice(1, 2))
        quantize_w1(0, slice(2, 4))
        reorder_w4(1)
        for half in range(HALVES):
            for t in range(PACK):
                layer_pass(group0[half][t], 0, t, half, 0, False, True)
        for t in range(PACK):
            relu_out(group0[0][t], 0, t, 0)

        round_w1(1, nc.vector.tensor_copy, slice(0, P // 2))
        round_w1(2, nc.vector.tensor_copy, slice(0, P // 2))
        quantize_w1(1, slice(0, 1))
        quantize_w1(1, slice(1, 2))
        quantize_w1(1, slice(2, PACK))

        def open_group1(acc, t, half):
            for a in range(1, USER_PASSES):
                layer_pass(acc, 1, t, half, a, a == 1, False)

        def close_group1(acc, t, half):
            layer_pass(acc, 1, t, half, 0, False, True)
            relu_out(acc, 1, t, half)

        sums = [bank(t) for t in range(PACK)]
        for t in range(PACK + 2):
            if t < PACK:
                open_group1(sums[t], t, 0)
            if t >= 2:
                close_group1(sums[t - 2], t - 2, 0)
        for t in range(PACK):
            relu_out(group0[1][t], 0, t, 1)
        quantize_h(0, 0)
        early_items = sbuf("early_items", [P, 2 * ITEM_CHUNK], U32, "shared_h")
        item_words = {(0, chunk): early_items[:, chunk * ITEM_CHUNK : (chunk + 1) * ITEM_CHUNK] for chunk in range(2)}
        sums = [bank(PACK + t) for t in range(PACK)]
        for t in range(PACK):
            open_group1(sums[t], t, 1)
            close_group1(sums[t], t, 1)

        item_chunks = [(first, ITEM_CHUNK) for first in range(0, S2, ITEM_CHUNK)]

        def gather_items(words, g, first, count):
            nc.vector.tensor_copy(words, item_table[g][:].bitcast(U32).indirect(entries(items, first, count)))

        def gather_late(g, chunk):
            words = placed.tile(
                [P, ITEM_CHUNK], U32, name="item_words%d_%d" % (g, chunk), align_bytes=256, offset=LATE + (len(item_words) - 3) * ITEM_CHUNK * BYTES
            )
            item_words[g, chunk] = words[:]
            gather_items(words[:], g, chunk * ITEM_CHUNK, ITEM_CHUNK)

        def score(sums, tiles, half, columns):
            count = columns.stop - columns.start
            prob = results.tile([P, len(tiles), count], F32, name="prob", align_bytes=256)
            for n, i in enumerate(tiles):
                part = max(c for c, (first, size) in enumerate(item_chunks) if first <= i * P)
                at = i * P - item_chunks[part][0]
                for g in range(GROUPS):
                    nc.tensor.matmul_mx(
                        out=sums[i][:, columns],
                        lhsT=item_words[g, part][:, at : at + P].bitcast(FP8X4),
                        lhsT_scale=item_plane[ITEM_SHIFT:P, g, :].bitcast(U8)[:, i * P : (i + 1) * P],
                        rhs=h_codes[g, half][:, columns].bitcast(FP8X4),
                        rhs_scale=h_plane[g, half][:, columns],
                        start=g == 0,
                        stop=g == GROUPS - 1,
                    )
                nc.scalar.activation(prob[:, n, :], sums[i][:, columns], ACT.Sigmoid, bias=b2_cols[:, i : i + 1])
            rows = out[tiles[0] * P : (tiles[-1] + 1) * P, half * BANK + columns.start : half * BANK + columns.stop]
            nc.sync.dma_start(rows.rearrange("(n p) c -> p n c", p=P), prob[:])

        def in_pairs(tiles):
            return [tiles[n : n + 2] for n in range(0, len(tiles), 2)]

        whole = slice(0, BANK)
        gather_items(early_items[:], 0, 0, 2 * ITEM_CHUNK)
        first_items = placed.tile([P, ITEM_CHUNK], U32, name="first_items", align_bytes=256, offset=T * BYTES + 2048)
        item_words[1, 0] = first_items[:]
        gather_items(first_items[:], 1, 0, ITEM_CHUNK)
        quantize_h(1, 0)
        for chunk, (first, count) in enumerate(item_chunks):
            for g in range(GROUPS):
                if (g, chunk) not in item_words:
                    gather_late(g, chunk)
            tiles = list(range(first // P, (first + count) // P))
            sums = {i: bank(i) for i in tiles}
            for pair in ([[0], [1]] if chunk == 0 else in_pairs(tiles)):
                score(sums, pair, 0, whole)
        h_packed[0, 1] = placed.tile([P, BANK * PACK], BF16, name="h_packed0_1", align_bytes=256, offset=0)
        h_packed[1, 1] = sbuf("h_packed1_1", [P, BANK * PACK], BF16)
        sums = [bank(i) for i in range(ITEM_TILES)]
        for s in range(PIECES):
            for g in range(GROUPS):
                interleave_h(g, 1, s)
            for g in range(GROUPS):
                quantize_piece(g, 1, s)
            if s == 0:
                for pair in in_pairs(list(range(SPLIT_TILES))):
                    score(sums, pair, 1, slice(0, width))
        for i in range(SPLIT_TILES, ITEM_TILES):
            score(sums, [i], 1, whole)
        for pair in in_pairs(list(range(SPLIT_TILES - 2))) + [[SPLIT_TILES - 2], [SPLIT_TILES - 1]]:
            score(sums, pair, 1, slice(width, BANK))
